import numpy as np
import ml_dtypes


def mxq(x, axis, fmt="e4m3"):
    dtype, down = {"e4m3": (ml_dtypes.float8_e4m3fn, 7), "e5m2": (ml_dtypes.float8_e5m2, 14)}[fmt]
    v = np.moveaxis(np.asarray(x, np.float32).astype(ml_dtypes.bfloat16).astype(np.float64), axis, -1)
    blocks = v.reshape(v.shape[:-1] + (-1, 32))
    amax = np.abs(blocks).max(-1, keepdims=True)
    byte = np.maximum(np.where(amax > 0, np.frexp(amax)[1] - 1 + 127, 0) - down, 1)
    scale = np.exp2(byte - 127.0)
    codes = (blocks / scale).astype(np.float32).astype(dtype).astype(np.float64)
    return np.moveaxis((codes * scale).reshape(v.shape), -1, axis)


WIDE = False


def mx_kscale(k):
    if not WIDE:
        return np.ones(k)
    levels = np.array([10, -10, 5, -5, 0])
    if k % 512:
        return np.exp2(np.random.permutation(np.resize(levels, k // 32))).repeat(32)
    a = np.empty((k // 512, 16))
    for p in range(k // 512):
        a[p, :8] = np.random.permutation(np.resize(levels, 8))
        for g in range(8):
            far = levels[np.abs(levels - a[p, g]) >= 10]
            a[p, g + 8] = far[np.random.randint(len(far))]
    return np.exp2(a.ravel()).repeat(32)


def f64(x):
    return np.asarray(x).astype(np.float64)


def striped8(idx):
    return np.concatenate([x.reshape(-1, 16).T for x in idx]).astype(np.uint16)


def runs(offs, k):
    lists = np.stack([offs[16 * r : 16 * r + 16].T.reshape(-1) for r in range(8)]).astype(np.int64)
    return lists[np.arange(k) % 512 // 64]


def pack_weight(w):
    k, n = w.shape
    w = f64(np.asarray(w, np.float32).astype(ml_dtypes.bfloat16)).reshape(k // 32, 32, n)
    amax = np.abs(w).max(1)
    byte = np.clip(np.where(amax > 0, np.frexp(amax)[1] - 1 + 127 - 7, 1), 1, 254)
    scaled = (w * np.exp2(127.0 - byte)[:, None, :]).reshape(k, n).astype(np.float32)
    words = np.ascontiguousarray(scaled.reshape(k // 512, 128, 4, n).transpose(0, 1, 3, 2)).astype(ml_dtypes.float8_e4m3fn).view(np.uint8)
    return words, np.ascontiguousarray(byte.astype(np.uint8).reshape(k // 512, 16, n))


def unpack_weight(words, scales):
    g, p, n, _ = words.shape
    vals = np.ascontiguousarray(words).view(ml_dtypes.float8_e4m3fn).astype(np.float64) * np.repeat(np.exp2(scales.astype(np.float64) - 127.0), 8, axis=1)[..., None]
    return vals.transpose(0, 1, 3, 2).reshape(g * 512, n)


K, T, S, N, H, U = 512, 2048, 512, 512, 512, 512


def setup_inputs():
    n = np.random.standard_normal
    s = mx_kscale(K)[:, None]
    u = mx_kscale(H)
    packed_xT = pack_weight(n((K, T)) * s)
    return {
        "x_words": packed_xT[0],
        "x_scales": packed_xT[1],
        "w1": (n((K, H)) / np.sqrt(K) / s * u).astype(np.float32),
        "kern1": n((H, U)).astype(np.float32),
        "kern2": n((H, U)).astype(np.float32),
        "w2": (n((H, N)) / np.sqrt(H) / u[:, None]).astype(np.float32),
        "offs": striped8(np.stack([np.random.permutation(T)[:S] for _ in range(8)])),
        "cls": striped8(np.random.randint(0, U, (8, S))),
        "p1": striped8(np.stack([np.random.permutation(S) for _ in range(8)])),
        "p2": striped8(np.stack([np.random.permutation(S) for _ in range(8)])),
    }


def reference(x_words, x_scales, w1, kern1, kern2, w2, offs, cls, p1, p2):
    k1 = f64(kern1)[np.arange(H)[:, None], runs(cls, H)]
    xq = unpack_weight(x_words, x_scales)[np.arange(K)[:, None], runs(offs, K)]
    y = mxq(f64(w1), 0, "e4m3").T @ xq
    k2 = f64(kern2)[np.arange(H)[:, None], runs(cls, H)]
    z = k1 * (y[np.arange(H)[:, None], runs(p1, H)]) + k2 * (y[np.arange(H)[:, None], runs(p2, H)])
    return mxq(f64(w2), 0, "e4m3").T @ mxq(z, 0, "e4m3")

@@ -1,0 +1,200 @@
+from contextlib import ExitStack
+
+import concourse.mybir as mybir
+
+K, T, S, N, H, U = 512, 2048, 512, 512, 512, 512
+FLOPS = 2 * K * H * S + 2 * H * N * S
+
+F32 = mybir.dt.float32
+BF16 = mybir.dt.bfloat16
+I32 = mybir.dt.int32
+U32 = mybir.dt.uint32
+U16 = mybir.dt.uint16
+U8 = mybir.dt.uint8
+FP8X4 = mybir.dt.float8_e4m3fn_x4
+MULT = mybir.AluOpType.mult
+ADD = mybir.AluOpType.add
+P = 128
+CHUNKS = (384, 128)
+KW = 1024
+
+
+def tile_picked_dynk8_none_p_kernel(
+    tc, x_words, x_scales, w1, kern1, kern2, w2, offs, cls, p1, p2, out
+):
+    nc = tc.nc
+    with ExitStack() as ctx:
+        lists = ctx.enter_context(tc.tile_pool(name="lists", bufs=1))
+        keep = ctx.enter_context(tc.tile_pool(name="keep", bufs=1))
+        psum = ctx.enter_context(tc.psum_pool(name="psum", bufs=1))
+
+        offs_t = lists.tile([P, S // 16], U16, name="offs_t")
+        cls_t = lists.tile([P, S // 16], U16, name="cls_t")
+        p1_t = lists.tile([P, S // 16], U16, name="p1_t")
+        p2_t = lists.tile([P, S // 16], U16, name="p2_t")
+
+        k1_win = [keep.tile([P, KW], F32, name=f"k1_win{t}") for t in range(4)]
+        k2_win = [keep.tile([P, KW], F32, name=f"k2_win{t}") for t in range(4)]
+        k1_rows = kern1.rearrange("(p t) u -> t p u", t=4)
+        k2_rows = kern2.rearrange("(p t) u -> t p u", t=4)
+        xs_win = keep.tile([P, T], U8, name="xs_win")
+        xw_win = keep.tile([P, T], U32, name="xw_win")
+        w1_raw = [keep.tile([P, 4, H // 2], F32, name=f"w1_raw{h}") for h in range(2)]
+        w2_raw = keep.tile([P, 4, N], F32, name="w2_raw")
+        w1_rows = w1.rearrange("(p j) c -> p j c", j=4)
+        scale_rows = x_scales[0].bitcast(I32).rearrange("(r e) c -> e r c", e=2)
+
+        def load_k(win, rows, t):
+            nc.sync.dma_start(out=win[t][:, 0:U], in_=rows[t])
+
+        nc.sync.dma_start(cls_t[:], cls)
+        load_k(k1_win, k1_rows, 0)
+        nc.sync.dma_start(offs_t[:], offs)
+        for e in range(2):
+            nc.sync.dma_start(
+                out=xs_win[e:P:2, :].bitcast(I32),
+                in_=scale_rows[e].unsqueeze(1).to_broadcast([8, 8, T // 4]),
+            )
+        load_k(k1_win, k1_rows, 1)
+        load_k(k1_win, k1_rows, 2)
+        nc.sync.dma_start(
+            out=xw_win[:].bitcast(I32),
+            in_=x_words[0].rearrange("p n t -> p (n t)").bitcast(I32),
+        )
+        nc.sync.dma_start(out=w1_raw[0][:], in_=w1_rows[:, :, 0 : H // 2])
+        load_k(k1_win, k1_rows, 3)
+        nc.sync.dma_start(out=w1_raw[1][:], in_=w1_rows[:, :, H // 2 : H])
+        for t in range(4):
+            load_k(k2_win, k2_rows, t)
+        nc.sync.dma_start(p1_t[:], p1)
+        nc.sync.dma_start(p2_t[:], p2)
+        nc.sync.dma_start(out=w2_raw[:], in_=w2.rearrange("(p j) c -> p j c", j=4))
+
+        xq_scales = keep.tile([P, S], U8, name="xq_scales", align_bytes=64)
+        nc.vector.memset(xq_scales[:].bitcast(I32), 0)
+
+
+        k1g = [None] * 4
+        k2g = [None] * 4
+
+        def gather_k(dst, win, t, tag):
+            dst[t] = keep.tile([P, S], F32, name=tag, tag=tag, align_bytes=64)
+            nc.vector.tensor_copy(dst[t][:], win[t][:].indirect(cls_t[:]))
+
+        gather_k(k1g, k1_win, 0, "k1g0")
+        xs_got = keep.tile([P, S], U8, name="xs_got", align_bytes=64)
+        nc.vector.tensor_copy(xs_got[:], xs_win[:].indirect(offs_t[:]))
+        nc.scalar.dma_start(out=xq_scales[0:100, :].bitcast(I32), in_=xs_got[14:114, :].bitcast(I32))
+        gather_k(k1g, k1_win, 1, "k1g1")
+        gather_k(k1g, k1_win, 2, "k1g2")
+        xq_words = keep.tile([P, S], U32, name="xq_words", align_bytes=64)
+        nc.vector.tensor_copy(xq_words[:], xw_win[:].indirect(offs_t[:]))
+        gather_k(k1g, k1_win, 3, "k1g3")
+
+        w1_bf = keep.tile([P, 4, P, 4], BF16, name="w1_bf", tag="w1_bf", align_bytes=64)
+        for h in range(2):
+            nc.scalar.copy(
+                out=w1_bf[:, :, 64 * h : 64 * (h + 1), :].rearrange("p t m j -> p m j t"),
+                in_=w1_raw[h][:].rearrange("p j (m t) -> p m j t", t=4),
+            )
+        gather_k(k2g, k2_win, 0, "k2g0")
+        gather_k(k2g, k2_win, 1, "k2g1")
+        w1_codes = keep.tile([P, H], U32, name="w1_codes", align_bytes=64)
+        w1_scales = keep.tile([P, H], U8, name="w1_scales", align_bytes=64)
+        nc.vector.quantize_mx(
+            out=w1_codes[:].bitcast(FP8X4), scales=w1_scales[:], in_=w1_bf[:].rearrange("p t m j -> p (t m j)")
+        )
+        banks = [psum.tile([P, 512], F32, name=f"ybank{t}", tag=f"ybank{t}") for t in range(4)]
+        y_win = [keep.tile([P, S], F32, name=f"y_win{t}") for t in range(4)]
+        for t in range(4):
+            nc.tensor.matmul_mx(
+                out=banks[t][:],
+                lhsT=w1_codes[:, P * t : P * (t + 1)].bitcast(FP8X4),
+                lhsT_scale=w1_scales[:, P * t : P * (t + 1)],
+                rhs=xq_words[:].bitcast(FP8X4),
+                rhs_scale=xq_scales[:],
+                start=True,
+                stop=True,
+            )
+            nc.scalar.copy(out=y_win[t][:], in_=banks[t][:])
+        gather_k(k2g, k2_win, 2, "w1_bf")
+        gather_k(k2g, k2_win, 3, "k2g3")
+
+        w2_bf = keep.tile([P, N, 4], BF16, name="w2_bf", align_bytes=64)
+        nc.scalar.copy(
+            out=w2_bf[:].rearrange("p (c i) j -> p c j i", i=4),
+            in_=w2_raw[:].rearrange("p j (c i) -> p c j i", i=4),
+        )
+        w2_codes = keep.tile([P, N], U32, name="w2_codes", align_bytes=64)
+        w2_scales = keep.tile([P, N], U8, name="w2_scales", align_bytes=64)
+
+        out_rows = out.rearrange("(mt p) j -> p mt j", p=P)
+
+        def products(c, a, n, t, tag):
+            cols = slice(a // 16, (a + n) // 16)
+            prod1 = keep.tile([P, n], F32, name=f"prod1_{c}_{t}", tag=tag, align_bytes=64)
+            prod2 = keep.tile([P, n], F32, name=f"prod2_{c}_{t}")
+            nc.vector.tensor_tensor(prod1[:], y_win[t][:].indirect(p1_t[:, cols]), k1g[t][:, a : a + n], MULT)
+            nc.vector.tensor_tensor(prod2[:], y_win[t][:].indirect(p2_t[:, cols]), k2g[t][:, a : a + n], MULT)
+            return prod1, prod2
+
+        def interleave(copy, planes, b, m, name):
+            z_bf = keep.tile([P, m, 4], BF16, name=name, tag=name, align_bytes=64)
+            copy(
+                z_bf[:].rearrange("p (c i) t -> p c t i", i=4),
+                planes[:, :, b : b + m].rearrange("p t (c i) -> p c t i", i=4),
+            )
+            return z_bf
+
+        def finish(z_bf, a, m, last):
+            z_codes = keep.tile([P, m], U32, name=f"z_codes{a}", align_bytes=64)
+            z_scales = keep.tile([P, m], U8, name=f"z_scales{a}", align_bytes=64)
+            nc.vector.quantize_mx(
+                out=z_codes[:].bitcast(FP8X4), scales=z_scales[:], in_=z_bf[:].rearrange("p n j -> p (n j)")
+            )
+            per_bank = 2 if (last or m == 256) else 4
+            for g in range(4 // per_bank):
+                acc = psum.tile([P, per_bank, m], F32, name=f"obank{a}_{g}", tag=("ybank" if last else "obank") + str(g + (2 if m == 128 and not last else 0)))
+                res = keep.tile([P, per_bank, m], F32, name=f"res{a}_{g}")
+                for q in range(per_bank):
+                    mt = per_bank * g + q
+                    nc.tensor.matmul_mx(
+                        out=acc[:, q, :],
+                        lhsT=w2_codes[:, P * mt : P * (mt + 1)].bitcast(FP8X4),
+                        lhsT_scale=w2_scales[:, P * mt : P * (mt + 1)],
+                        rhs=z_codes[:].bitcast(FP8X4),
+                        rhs_scale=z_scales[:],
+                        start=True,
+                        stop=True,
+                    )
+                dst = out_rows[:, per_bank * g : per_bank * (g + 1), a : a + m]
+                if last and g == 1:
+                    nc.vector.tensor_copy(res[:], acc[:])
+                    nc.sync.dma_start(out=dst, in_=res[:])
+                elif last:
+                    nc.scalar.copy(res[:], acc[:])
+                    nc.scalar.dma_start(out=dst, in_=res[:])
+                else:
+                    nc.scalar.copy(res[:], acc[:])
+                    nc.sync.dma_start(out=dst, in_=res[:])
+
+        planes0 = keep.tile([P, 4, 384], BF16, name="planes0")
+        planes1 = keep.tile([P, 4, 128], BF16, name="planes1")
+        for t in range(4):
+            prod1, prod2 = products(0, 0, 384, t, f"first{t}")
+            if t == 1:
+                nc.vector.quantize_mx(
+                    out=w2_codes[:].bitcast(FP8X4), scales=w2_scales[:], in_=w2_bf[:].rearrange("p n j -> p (n j)")
+                )
+            nc.vector.tensor_tensor(planes0[:, t, :], prod1[:], prod2[:], ADD)
+        z_a = interleave(nc.scalar.copy, planes0, 0, 256, "z_a")
+        z_b = interleave(nc.scalar.copy, planes0, 256, 128, "z_b")
+        for t in range(4):
+            if t == 2:
+                finish(z_a, 0, 256, False)
+            if t == 3:
+                finish(z_b, 256, 128, False)
+            prod1, prod2 = products(1, 384, 128, t, ["second0", "second1", "z_a", "z_b"][t])
+            nc.vector.tensor_tensor(planes1[:, t, :], prod1[:], prod2[:], ADD)
+        z_c = interleave(nc.vector.tensor_copy, planes1, 0, 128, "z_c")
+        finish(z_c, 384, 128, True)

@@ -1,6 +1,7 @@
 from contextlib import ExitStack
 
 import concourse.mybir as mybir
+from concourse.masks import make_identity
 
 K, T, S, N, H, U = 512, 2048, 512, 512, 512, 512
 FLOPS = 2 * K * H * S + 2 * H * N * S
@@ -35,14 +36,15 @@ def tile_picked_dynk8_none_p_kernel(
 
         k1_win = [keep.tile([P, KW], F32, name=f"k1_win{t}") for t in range(4)]
         k2_win = [keep.tile([P, KW], F32, name=f"k2_win{t}") for t in range(4)]
-        k1_rows = kern1.rearrange("(p t) u -> t p u", t=4)
-        k2_rows = kern2.rearrange("(p t) u -> t p u", t=4)
+        k1_rows = kern1.rearrange("(g t f) u -> t g f u", t=4, f=4)
+        k2_rows = kern2.rearrange("(g t f) u -> t g f u", t=4, f=4)
         xs_win = keep.tile([P, T], U8, name="xs_win")
         xw_win = keep.tile([P, T], U32, name="xw_win")
         w1_raw = [keep.tile([P, 4, H // 2], F32, name=f"w1_raw{h}") for h in range(2)]
         w2_raw = keep.tile([P, 4, N], F32, name="w2_raw")
         w1_rows = w1.rearrange("(p j) c -> p j c", j=4)
-        scale_rows = x_scales[0].bitcast(I32).rearrange("(r e) c -> e r c", e=2)
+        w2_rows = w2.rearrange("(g t f) u -> t g f u", t=4, f=4)
+        nc.gpsimd.memset(xs_win[:].bitcast(I32), 0)
 
         def load_k(win, rows, t):
             nc.sync.dma_start(out=win[t][:, 0:U], in_=rows[t])
@@ -50,11 +52,7 @@ def tile_picked_dynk8_none_p_kernel(
         nc.sync.dma_start(cls_t[:], cls)
         load_k(k1_win, k1_rows, 0)
         nc.sync.dma_start(offs_t[:], offs)
-        for e in range(2):
-            nc.sync.dma_start(
-                out=xs_win[e:P:2, :].bitcast(I32),
-                in_=scale_rows[e].unsqueeze(1).to_broadcast([8, 8, T // 4]),
-            )
+        nc.sync.dma_start(out=xs_win[0:P:8, :].bitcast(I32), in_=x_scales[0].bitcast(I32))
         load_k(k1_win, k1_rows, 1)
         load_k(k1_win, k1_rows, 2)
         nc.sync.dma_start(
@@ -68,10 +66,13 @@ def tile_picked_dynk8_none_p_kernel(
             load_k(k2_win, k2_rows, t)
         nc.sync.dma_start(p1_t[:], p1)
         nc.sync.dma_start(p2_t[:], p2)
-        nc.sync.dma_start(out=w2_raw[:], in_=w2.rearrange("(p j) c -> p j c", j=4))
+        for t in range(4):
+            nc.sync.dma_start(out=w2_raw[:, t, :], in_=w2_rows[t])
 
         xq_scales = keep.tile([P, S], U8, name="xq_scales", align_bytes=64)
-        nc.vector.memset(xq_scales[:].bitcast(I32), 0)
+        nc.gpsimd.memset(xq_scales[:].bitcast(I32), 0)
+        ident = keep.tile([P, P], F32, name="ident")
+        make_identity(nc, ident[:])
 
 
         k1g = [None] * 4
@@ -84,7 +85,8 @@ def tile_picked_dynk8_none_p_kernel(
         gather_k(k1g, k1_win, 0, "k1g0")
         xs_got = keep.tile([P, S], U8, name="xs_got", align_bytes=64)
         nc.vector.tensor_copy(xs_got[:], xs_win[:].indirect(offs_t[:]))
-        nc.scalar.dma_start(out=xq_scales[0:100, :].bitcast(I32), in_=xs_got[14:114, :].bitcast(I32))
+        for r in range(4):
+            nc.scalar.dma_start(out=xq_scales[r:P:32, :].bitcast(I32), in_=xs_got[8 * r : P : 32, :].bitcast(I32))
         gather_k(k1g, k1_win, 1, "k1g1")
         gather_k(k1g, k1_win, 2, "k1g2")
         xq_words = keep.tile([P, S], U32, name="xq_words", align_bytes=64)
@@ -94,8 +96,8 @@ def tile_picked_dynk8_none_p_kernel(
         w1_bf = keep.tile([P, 4, P, 4], BF16, name="w1_bf", tag="w1_bf", align_bytes=64)
         for h in range(2):
             nc.scalar.copy(
-                out=w1_bf[:, :, 64 * h : 64 * (h + 1), :].rearrange("p t m j -> p m j t"),
-                in_=w1_raw[h][:].rearrange("p j (m t) -> p m j t", t=4),
+                out=w1_bf[:, :, 64 * h : 64 * (h + 1), :].rearrange("p t (g f) j -> p t g j f", f=4),
+                in_=w1_raw[h][:].rearrange("p j (g t f) -> p t g j f", t=4, f=4),
             )
         gather_k(k2g, k2_win, 0, "k2g0")
         gather_k(k2g, k2_win, 1, "k2g1")
@@ -104,7 +106,7 @@ def tile_picked_dynk8_none_p_kernel(
         nc.vector.quantize_mx(
             out=w1_codes[:].bitcast(FP8X4), scales=w1_scales[:], in_=w1_bf[:].rearrange("p t m j -> p (t m j)")
         )
-        banks = [psum.tile([P, 512], F32, name=f"ybank{t}", tag=f"ybank{t}") for t in range(4)]
+        banks = [psum.tile([P, 512], F32, name=f"ybank{t}", tag=f"bank{t}") for t in range(4)]
         y_win = [keep.tile([P, S], F32, name=f"y_win{t}") for t in range(4)]
         for t in range(4):
             nc.tensor.matmul_mx(
@@ -146,7 +148,7 @@ def tile_picked_dynk8_none_p_kernel(
             )
             return z_bf
 
-        def finish(z_bf, a, m, last):
+        def finish(z_bf, a, m, last, bank0):
             z_codes = keep.tile([P, m], U32, name=f"z_codes{a}", align_bytes=64)
             z_scales = keep.tile([P, m], U8, name=f"z_scales{a}", align_bytes=64)
             nc.vector.quantize_mx(
@@ -154,7 +156,7 @@ def tile_picked_dynk8_none_p_kernel(
             )
             per_bank = 2 if (last or m == 256) else 4
             for g in range(4 // per_bank):
-                acc = psum.tile([P, per_bank, m], F32, name=f"obank{a}_{g}", tag=("ybank" if last else "obank") + str(g + (2 if m == 128 and not last else 0)))
+                acc = psum.tile([P, per_bank, m], F32, name=f"obank{a}_{g}", tag=f"bank{bank0 + g}")
                 res = keep.tile([P, per_bank, m], F32, name=f"res{a}_{g}")
                 for q in range(per_bank):
                     mt = per_bank * g + q
@@ -178,23 +180,44 @@ def tile_picked_dynk8_none_p_kernel(
                     nc.scalar.copy(res[:], acc[:])
                     nc.sync.dma_start(out=dst, in_=res[:])
 
-        planes0 = keep.tile([P, 4, 384], BF16, name="planes0")
         planes1 = keep.tile([P, 4, 128], BF16, name="planes1")
+        sums = [psum.tile([P, 4, P], F32, name=f"sums{jb}", tag=f"bank{4 + jb}") for jb in range(3)]
+        turned = [[keep.tile([P, P, 2], BF16, name=f"turned{jb}_{u}") for u in range(2)] for jb in range(3)]
+        back = [psum.tile([P, 2, 256], F32, name="back0", tag="bank7"), psum.tile([P, 2, 128], F32, name="back1", tag="bank0")]
         for t in range(4):
-            prod1, prod2 = products(0, 0, 384, t, f"first{t}")
+            prods = products(0, 0, 384, t, f"first{t}")
             if t == 1:
                 nc.vector.quantize_mx(
                     out=w2_codes[:].bitcast(FP8X4), scales=w2_scales[:], in_=w2_bf[:].rearrange("p n j -> p (n j)")
                 )
-            nc.vector.tensor_tensor(planes0[:, t, :], prod1[:], prod2[:], ADD)
-        z_a = interleave(nc.scalar.copy, planes0, 0, 256, "z_a")
-        z_b = interleave(nc.scalar.copy, planes0, 256, 128, "z_b")
+            for s in range(2):
+                for jb in range(3):
+                    nc.tensor.matmul(
+                        sums[jb][:, t, :], prods[s][:, P * jb : P * (jb + 1)], ident[:],
+                        start=(s == 0), stop=(s == 1), is_transpose=True,
+                    )
+            if t % 2 == 1:
+                u = t // 2
+                for jb in range(3):
+                    nc.scalar.copy(turned[jb][u][:], sums[jb][:, 2 * u : 2 * u + 2, :].rearrange("j e p -> j p e"))
+                for jb in range(3):
+                    nc.tensor.transpose(
+                        back[jb // 2][:, u, P * (jb % 2) : P * (jb % 2 + 1)],
+                        turned[jb][u][:].rearrange("j p e -> j (p e)").bitcast(F32),
+                        ident[:],
+                    )
+        z_a = keep.tile([P, 256, 4], BF16, name="z_a", tag="z_a", align_bytes=64)
+        z_b = keep.tile([P, 128, 4], BF16, name="z_b", tag="z_b", align_bytes=64)
+        for z_bf, bank in ((z_a, back[0]), (z_b, back[1])):
+            nc.scalar.copy(
+                z_bf[:].rearrange("p n j -> p (n j)").bitcast(F32).rearrange("p (n u) -> p n u", u=2),
+                bank[:].rearrange("p u n -> p n u"),
+            )
         for t in range(4):
-            if t == 2:
-                finish(z_a, 0, 256, False)
             if t == 3:
-                finish(z_b, 256, 128, False)
-            prod1, prod2 = products(1, 384, 128, t, ["second0", "second1", "z_a", "z_b"][t])
+                finish(z_a, 0, 256, False, 1)
+                finish(z_b, 256, 128, False, 3)
+            prod1, prod2 = products(1, 384, 128, t, ["second0", "second1", "second2", "z_a"][t])
             nc.vector.tensor_tensor(planes1[:, t, :], prod1[:], prod2[:], ADD)
         z_c = interleave(nc.vector.tensor_copy, planes1, 0, 128, "z_c")
-        finish(z_c, 384, 128, True)
+        finish(z_c, 384, 128, True, 4)

@@ -16,8 +16,8 @@ FP8X4 = mybir.dt.float8_e4m3fn_x4
 MULT = mybir.AluOpType.mult
 ADD = mybir.AluOpType.add
 P = 128
-CHUNKS = (384, 128)
-KW = 1024
+EARLY = 384
+LATE = S - EARLY
 
 
 def tile_picked_dynk8_none_p_kernel(
@@ -34,129 +34,151 @@ def tile_picked_dynk8_none_p_kernel(
         p1_t = lists.tile([P, S // 16], U16, name="p1_t")
         p2_t = lists.tile([P, S // 16], U16, name="p2_t")
 
-        k1_win = [keep.tile([P, KW], F32, name=f"k1_win{t}") for t in range(4)]
-        k2_win = [keep.tile([P, KW], F32, name=f"k2_win{t}") for t in range(4)]
-        k1_rows = kern1.rearrange("(g t f) u -> t g f u", t=4, f=4)
-        k2_rows = kern2.rearrange("(g t f) u -> t g f u", t=4, f=4)
+        k_win = [[keep.tile([P, 2 * U], F32, name=f"k_win{s}_{t}") for t in range(4)] for s in range(2)]
+        k_rows = [kern.rearrange("(g t f) u -> t g f u", t=4, f=4) for kern in (kern1, kern2)]
         xs_win = keep.tile([P, T], U8, name="xs_win")
         xw_win = keep.tile([P, T], U32, name="xw_win")
+        xw_rows = x_words[0].rearrange("p n t -> p (n t)").bitcast(I32)
         w1_raw = [keep.tile([P, 4, H // 2], F32, name=f"w1_raw{h}") for h in range(2)]
-        w2_raw = keep.tile([P, 4, N], F32, name="w2_raw")
         w1_rows = w1.rearrange("(p j) c -> p j c", j=4)
+        w2_raw = keep.tile([P, 4, N], F32, name="w2_raw")
         w2_rows = w2.rearrange("(g t f) u -> t g f u", t=4, f=4)
-        nc.gpsimd.memset(xs_win[:].bitcast(I32), 0)
+        xq_scales = keep.tile([P, S], U8, name="xq_scales", align_bytes=64)
+        ident = keep.tile([P, P], F32, name="ident")
+        nc.vector.memset(xs_win[:].bitcast(I32), 0)
+        nc.gpsimd.memset(xq_scales[:].bitcast(I32), 0)
+        make_identity(nc, ident[:])
 
-        def load_k(win, rows, t):
-            nc.sync.dma_start(out=win[t][:, 0:U], in_=rows[t])
+        def load_k(s, t):
+            nc.sync.dma_start(out=k_win[s][t][:, 0:U], in_=k_rows[s][t])
+
+        def load_words(h):
+            cols = slice(T // 2 * h, T // 2 * (h + 1))
+            nc.sync.dma_start(out=xw_win[:].bitcast(I32)[:, cols], in_=xw_rows[:, cols])
+
+        def load_w1(h):
+            nc.sync.dma_start(out=w1_raw[h][:], in_=w1_rows[:, :, H // 2 * h : H // 2 * (h + 1)])
 
         nc.sync.dma_start(cls_t[:], cls)
-        load_k(k1_win, k1_rows, 0)
+        load_k(0, 0)
         nc.sync.dma_start(offs_t[:], offs)
         nc.sync.dma_start(out=xs_win[0:P:8, :].bitcast(I32), in_=x_scales[0].bitcast(I32))
-        load_k(k1_win, k1_rows, 1)
-        load_k(k1_win, k1_rows, 2)
-        nc.sync.dma_start(
-            out=xw_win[:].bitcast(I32),
-            in_=x_words[0].rearrange("p n t -> p (n t)").bitcast(I32),
-        )
-        nc.sync.dma_start(out=w1_raw[0][:], in_=w1_rows[:, :, 0 : H // 2])
-        load_k(k1_win, k1_rows, 3)
-        nc.sync.dma_start(out=w1_raw[1][:], in_=w1_rows[:, :, H // 2 : H])
-        for t in range(4):
-            load_k(k2_win, k2_rows, t)
+        load_k(0, 1)
+        load_words(0)
+        load_k(0, 2)
+        load_words(1)
+        load_k(0, 3)
+        load_w1(0)
+        load_k(1, 0)
+        load_k(1, 1)
+        load_w1(1)
+        load_k(1, 2)
+        load_k(1, 3)
         nc.sync.dma_start(p1_t[:], p1)
         nc.sync.dma_start(p2_t[:], p2)
         for t in range(4):
             nc.sync.dma_start(out=w2_raw[:, t, :], in_=w2_rows[t])
 
-        xq_scales = keep.tile([P, S], U8, name="xq_scales", align_bytes=64)
-        nc.gpsimd.memset(xq_scales[:].bitcast(I32), 0)
-        ident = keep.tile([P, P], F32, name="ident")
-        make_identity(nc, ident[:])
+        k_got = [[None] * 4, [None] * 4]
 
+        def gather_k(s, t, tag):
+            k_got[s][t] = keep.tile([P, S], F32, name=f"k_got{s}_{t}", tag=tag, align_bytes=64)
+            nc.vector.tensor_copy(k_got[s][t][:], k_win[s][t][:].indirect(cls_t[:]))
 
-        k1g = [None] * 4
-        k2g = [None] * 4
-
-        def gather_k(dst, win, t, tag):
-            dst[t] = keep.tile([P, S], F32, name=tag, tag=tag, align_bytes=64)
-            nc.vector.tensor_copy(dst[t][:], win[t][:].indirect(cls_t[:]))
-
-        gather_k(k1g, k1_win, 0, "k1g0")
+        gather_k(0, 0, "k00")
         xs_got = keep.tile([P, S], U8, name="xs_got", align_bytes=64)
         nc.vector.tensor_copy(xs_got[:], xs_win[:].indirect(offs_t[:]))
         for r in range(4):
             nc.scalar.dma_start(out=xq_scales[r:P:32, :].bitcast(I32), in_=xs_got[8 * r : P : 32, :].bitcast(I32))
-        gather_k(k1g, k1_win, 1, "k1g1")
-        gather_k(k1g, k1_win, 2, "k1g2")
+        gather_k(0, 1, "k01")
+        gather_k(0, 2, "k02")
+        gather_k(0, 3, "k03")
         xq_words = keep.tile([P, S], U32, name="xq_words", align_bytes=64)
         nc.vector.tensor_copy(xq_words[:], xw_win[:].indirect(offs_t[:]))
-        gather_k(k1g, k1_win, 3, "k1g3")
+        gather_k(1, 0, "k10")
+        gather_k(1, 1, "k11")
 
-        w1_bf = keep.tile([P, 4, P, 4], BF16, name="w1_bf", tag="w1_bf", align_bytes=64)
+        w1_bf = [keep.tile([P, 2, P, 4], BF16, name=f"w1_bf{u}", tag=f"w1_bf{u}", align_bytes=64) for u in range(2)]
         for h in range(2):
-            nc.scalar.copy(
-                out=w1_bf[:, :, 64 * h : 64 * (h + 1), :].rearrange("p t (g f) j -> p t g j f", f=4),
-                in_=w1_raw[h][:].rearrange("p j (g t f) -> p t g j f", t=4, f=4),
-            )
-        gather_k(k2g, k2_win, 0, "k2g0")
-        gather_k(k2g, k2_win, 1, "k2g1")
-        w1_codes = keep.tile([P, H], U32, name="w1_codes", align_bytes=64)
-        w1_scales = keep.tile([P, H], U8, name="w1_scales", align_bytes=64)
-        nc.vector.quantize_mx(
-            out=w1_codes[:].bitcast(FP8X4), scales=w1_scales[:], in_=w1_bf[:].rearrange("p t m j -> p (t m j)")
-        )
-        banks = [psum.tile([P, 512], F32, name=f"ybank{t}", tag=f"bank{t}") for t in range(4)]
+            for u in range(2):
+                nc.scalar.copy(
+                    out=w1_bf[u][:, :, 64 * h : 64 * (h + 1), :].rearrange("p t (g f) j -> p t g j f", f=4),
+                    in_=w1_raw[h][:].rearrange("p j (g t f) -> p t g j f", t=4, f=4)[:, 2 * u : 2 * u + 2],
+                )
         y_win = [keep.tile([P, S], F32, name=f"y_win{t}") for t in range(4)]
-        for t in range(4):
-            nc.tensor.matmul_mx(
-                out=banks[t][:],
-                lhsT=w1_codes[:, P * t : P * (t + 1)].bitcast(FP8X4),
-                lhsT_scale=w1_scales[:, P * t : P * (t + 1)],
-                rhs=xq_words[:].bitcast(FP8X4),
-                rhs_scale=xq_scales[:],
-                start=True,
-                stop=True,
+        for u in range(2):
+            w1_codes = keep.tile([P, 2 * P], U32, name=f"w1_codes{u}", align_bytes=64)
+            w1_scales = keep.tile([P, 2 * P], U8, name=f"w1_scales{u}", align_bytes=64)
+            nc.vector.quantize_mx(
+                out=w1_codes[:].bitcast(FP8X4), scales=w1_scales[:], in_=w1_bf[u][:].rearrange("p t m j -> p (t m j)")
             )
-            nc.scalar.copy(out=y_win[t][:], in_=banks[t][:])
-        gather_k(k2g, k2_win, 2, "w1_bf")
-        gather_k(k2g, k2_win, 3, "k2g3")
+            for e in range(2):
+                t = 2 * u + e
+                bank = psum.tile([P, S], F32, name=f"ybank{t}", tag=f"bank{t}")
+                nc.tensor.matmul_mx(
+                    out=bank[:],
+                    lhsT=w1_codes[:, P * e : P * (e + 1)].bitcast(FP8X4),
+                    lhsT_scale=w1_scales[:, P * e : P * (e + 1)],
+                    rhs=xq_words[:].bitcast(FP8X4),
+                    rhs_scale=xq_scales[:],
+                    start=True,
+                    stop=True,
+                )
+                nc.scalar.copy(out=y_win[t][:], in_=bank[:])
+            gather_k(1, 2 + u, f"w1_bf{u}")
 
         w2_bf = keep.tile([P, N, 4], BF16, name="w2_bf", align_bytes=64)
         nc.scalar.copy(
             out=w2_bf[:].rearrange("p (c i) j -> p c j i", i=4),
             in_=w2_raw[:].rearrange("p j (c i) -> p c j i", i=4),
         )
-        w2_codes = keep.tile([P, N], U32, name="w2_codes", align_bytes=64)
+
+        def product(dst, s, t, a, n):
+            places = (p1_t, p2_t)[s][:, a // 16 : (a + n) // 16]
+            nc.vector.tensor_tensor(dst, y_win[t][:].indirect(places), k_got[s][t][:, a : a + n], MULT)
+
+        sums = [
+            [psum.tile([P, 2, P], F32, name=f"sums{u}_{jb}", tag=f"bank{4 * (1 - u) + jb}") for jb in range(3)]
+            for u in range(2)
+        ]
+        back = [
+            psum.tile([P, 2, 256], F32, name="back0", tag="bank7"),
+            psum.tile([P, 2, 128], F32, name="back1", tag="bank3"),
+        ]
+        for t in range(4):
+            for s in range(2):
+                prod = keep.tile([P, EARLY], F32, name=f"early{s}_{t}", tag=f"early{s}_{t}", align_bytes=64)
+                product(prod[:], s, t, 0, EARLY)
+                for jb in range(3):
+                    nc.tensor.matmul(
+                        sums[t // 2][jb][:, t % 2, :], prod[:, P * jb : P * (jb + 1)], ident[:],
+                        start=(s == 0), stop=(s == 1), is_transpose=True,
+                    )
+            if t % 2 == 1:
+                u = t // 2
+                for jb in range(3):
+                    turned = keep.tile([P, P, 2], BF16, name=f"turned{jb}_{u}")
+                    nc.scalar.copy(turned[:], sums[u][jb][:].rearrange("j e p -> j p e"))
+                    nc.tensor.transpose(
+                        back[jb // 2][:, u, P * (jb % 2) : P * (jb % 2 + 1)],
+                        turned[:].rearrange("j p e -> j (p e)").bitcast(F32),
+                        ident[:],
+                    )
+
+        w2_codes = keep.tile([P, N], U32, name="w2_codes", tag="early0_3", align_bytes=64)
         w2_scales = keep.tile([P, N], U8, name="w2_scales", align_bytes=64)
+        nc.vector.quantize_mx(
+            out=w2_codes[:].bitcast(FP8X4), scales=w2_scales[:], in_=w2_bf[:].rearrange("p n j -> p (n j)")
+        )
 
         out_rows = out.rearrange("(mt p) j -> p mt j", p=P)
 
-        def products(c, a, n, t, tag):
-            cols = slice(a // 16, (a + n) // 16)
-            prod1 = keep.tile([P, n], F32, name=f"prod1_{c}_{t}", tag=tag, align_bytes=64)
-            prod2 = keep.tile([P, n], F32, name=f"prod2_{c}_{t}")
-            nc.vector.tensor_tensor(prod1[:], y_win[t][:].indirect(p1_t[:, cols]), k1g[t][:, a : a + n], MULT)
-            nc.vector.tensor_tensor(prod2[:], y_win[t][:].indirect(p2_t[:, cols]), k2g[t][:, a : a + n], MULT)
-            return prod1, prod2
-
-        def interleave(copy, planes, b, m, name):
-            z_bf = keep.tile([P, m, 4], BF16, name=name, tag=name, align_bytes=64)
-            copy(
-                z_bf[:].rearrange("p (c i) t -> p c t i", i=4),
-                planes[:, :, b : b + m].rearrange("p t (c i) -> p c t i", i=4),
-            )
-            return z_bf
-
-        def finish(z_bf, a, m, last, bank0):
+        def finish(z_bf, a, m, per_bank, bank0, copies, queues):
             z_codes = keep.tile([P, m], U32, name=f"z_codes{a}", align_bytes=64)
             z_scales = keep.tile([P, m], U8, name=f"z_scales{a}", align_bytes=64)
-            nc.vector.quantize_mx(
-                out=z_codes[:].bitcast(FP8X4), scales=z_scales[:], in_=z_bf[:].rearrange("p n j -> p (n j)")
-            )
-            per_bank = 2 if (last or m == 256) else 4
+            nc.vector.quantize_mx(out=z_codes[:].bitcast(FP8X4), scales=z_scales[:], in_=z_bf)
             for g in range(4 // per_bank):
-                acc = psum.tile([P, per_bank, m], F32, name=f"obank{a}_{g}", tag=f"bank{bank0 + g}")
+                acc = psum.tile([P, per_bank, m], F32, name=f"acc{a}_{g}", tag=f"bank{bank0 + g}")
                 res = keep.tile([P, per_bank, m], F32, name=f"res{a}_{g}")
                 for q in range(per_bank):
                     mt = per_bank * g + q
@@ -169,55 +191,27 @@ def tile_picked_dynk8_none_p_kernel(
                         start=True,
                         stop=True,
                     )
-                dst = out_rows[:, per_bank * g : per_bank * (g + 1), a : a + m]
-                if last and g == 1:
-                    nc.vector.tensor_copy(res[:], acc[:])
-                    nc.sync.dma_start(out=dst, in_=res[:])
-                elif last:
-                    nc.scalar.copy(res[:], acc[:])
-                    nc.scalar.dma_start(out=dst, in_=res[:])
-                else:
-                    nc.scalar.copy(res[:], acc[:])
-                    nc.sync.dma_start(out=dst, in_=res[:])
+                copies[g](res[:], acc[:])
+                queues[g].dma_start(out=out_rows[:, per_bank * g : per_bank * (g + 1), a : a + m], in_=res[:])
 
-        planes1 = keep.tile([P, 4, 128], BF16, name="planes1")
-        sums = [psum.tile([P, 4, P], F32, name=f"sums{jb}", tag=f"bank{4 + jb}") for jb in range(3)]
-        turned = [[keep.tile([P, P, 2], BF16, name=f"turned{jb}_{u}") for u in range(2)] for jb in range(3)]
-        back = [psum.tile([P, 2, 256], F32, name="back0", tag="bank7"), psum.tile([P, 2, 128], F32, name="back1", tag="bank0")]
-        for t in range(4):
-            prods = products(0, 0, 384, t, f"first{t}")
-            if t == 1:
-                nc.vector.quantize_mx(
-                    out=w2_codes[:].bitcast(FP8X4), scales=w2_scales[:], in_=w2_bf[:].rearrange("p n j -> p (n j)")
-                )
-            for s in range(2):
-                for jb in range(3):
-                    nc.tensor.matmul(
-                        sums[jb][:, t, :], prods[s][:, P * jb : P * (jb + 1)], ident[:],
-                        start=(s == 0), stop=(s == 1), is_transpose=True,
-                    )
-            if t % 2 == 1:
-                u = t // 2
-                for jb in range(3):
-                    nc.scalar.copy(turned[jb][u][:], sums[jb][:, 2 * u : 2 * u + 2, :].rearrange("j e p -> j p e"))
-                for jb in range(3):
-                    nc.tensor.transpose(
-                        back[jb // 2][:, u, P * (jb % 2) : P * (jb % 2 + 1)],
-                        turned[jb][u][:].rearrange("j p e -> j (p e)").bitcast(F32),
-                        ident[:],
-                    )
-        z_a = keep.tile([P, 256, 4], BF16, name="z_a", tag="z_a", align_bytes=64)
-        z_b = keep.tile([P, 128, 4], BF16, name="z_b", tag="z_b", align_bytes=64)
-        for z_bf, bank in ((z_a, back[0]), (z_b, back[1])):
-            nc.scalar.copy(
-                z_bf[:].rearrange("p n j -> p (n j)").bitcast(F32).rearrange("p (n u) -> p n u", u=2),
-                bank[:].rearrange("p u n -> p n u"),
-            )
+        z_a = keep.tile([P, 512], F32, name="z_a", tag="z_a", align_bytes=64)
+        z_b = keep.tile([P, 256], F32, name="z_b", align_bytes=64)
+        nc.scalar.copy(z_a[:].rearrange("p (n u) -> p n u", u=2), back[0][:].rearrange("p u n -> p n u"))
+        nc.scalar.copy(z_b[:].rearrange("p (n u) -> p n u", u=2), back[1][:].rearrange("p u n -> p n u"))
+        planes = keep.tile([P, 4, LATE], BF16, name="planes")
         for t in range(4):
             if t == 3:
-                finish(z_a, 0, 256, False, 1)
-                finish(z_b, 256, 128, False, 3)
-            prod1, prod2 = products(1, 384, 128, t, ["second0", "second1", "second2", "z_a"][t])
-            nc.vector.tensor_tensor(planes1[:, t, :], prod1[:], prod2[:], ADD)
-        z_c = interleave(nc.vector.tensor_copy, planes1, 0, 128, "z_c")
-        finish(z_c, 384, 128, True, 4)
+                finish(z_a[:].bitcast(BF16), 0, 256, 2, 4, [nc.scalar.copy] * 2, [nc.sync] * 2)
+                finish(z_b[:].bitcast(BF16), 256, 128, 4, 6, [nc.scalar.copy], [nc.sync])
+            late = keep.tile([P, 2, LATE], F32, name=f"late{t}", tag="z_a" if t == 3 else f"late{t}", align_bytes=64)
+            for s in range(2):
+                product(late[:, s, :], s, t, EARLY, LATE)
+            nc.vector.tensor_tensor(planes[:, t, :], late[:, 0, :], late[:, 1, :], ADD)
+        z_c = keep.tile([P, LATE, 4], BF16, name="z_c", align_bytes=64)
+        nc.vector.tensor_copy(
+            z_c[:].rearrange("p (c i) t -> p c t i", i=4), planes[:].rearrange("p t (c i) -> p c t i", i=4)
+        )
+        finish(
+            z_c[:].rearrange("p n t -> p (n t)"), EARLY, LATE, 1, 0,
+            [nc.scalar.copy, nc.vector.tensor_copy] * 2, [nc.sync, nc.sync, nc.scalar, nc.sync],
+        )

@@ -39,39 +39,30 @@ def tile_picked_dynk8_none_p_kernel(
         xs_win = keep.tile([P, T], U8, name="xs_win")
         xw_win = keep.tile([P, T], U32, name="xw_win")
         xw_rows = x_words[0].rearrange("p n t -> p (n t)").bitcast(I32)
-        w1_raw = [keep.tile([P, 4, H // 2], F32, name=f"w1_raw{h}") for h in range(2)]
+        w1_raw = keep.tile([P, 4, H], F32, name="w1_raw")
         w1_rows = w1.rearrange("(p j) c -> p j c", j=4)
         w2_raw = keep.tile([P, 4, N], F32, name="w2_raw")
         w2_rows = w2.rearrange("(g t f) u -> t g f u", t=4, f=4)
         xq_scales = keep.tile([P, S], U8, name="xq_scales", align_bytes=64)
         ident = keep.tile([P, P], F32, name="ident")
-        nc.vector.memset(xs_win[:].bitcast(I32), 0)
+        nc.gpsimd.memset(xs_win[:].bitcast(I32), 0)
         nc.gpsimd.memset(xq_scales[:].bitcast(I32), 0)
         make_identity(nc, ident[:])
 
         def load_k(s, t):
             nc.sync.dma_start(out=k_win[s][t][:, 0:U], in_=k_rows[s][t])
 
-        def load_words(h):
-            cols = slice(T // 2 * h, T // 2 * (h + 1))
-            nc.sync.dma_start(out=xw_win[:].bitcast(I32)[:, cols], in_=xw_rows[:, cols])
-
-        def load_w1(h):
-            nc.sync.dma_start(out=w1_raw[h][:], in_=w1_rows[:, :, H // 2 * h : H // 2 * (h + 1)])
-
         nc.sync.dma_start(cls_t[:], cls)
         load_k(0, 0)
         nc.sync.dma_start(offs_t[:], offs)
-        nc.sync.dma_start(out=xs_win[0:P:8, :].bitcast(I32), in_=x_scales[0].bitcast(I32))
         load_k(0, 1)
-        load_words(0)
+        nc.sync.dma_start(out=xs_win[0:P:8, :].bitcast(I32), in_=x_scales[0].bitcast(I32))
         load_k(0, 2)
-        load_words(1)
         load_k(0, 3)
-        load_w1(0)
+        nc.sync.dma_start(out=w1_raw[:], in_=w1_rows)
         load_k(1, 0)
         load_k(1, 1)
-        load_w1(1)
+        nc.sync.dma_start(out=xw_win[:].bitcast(I32), in_=xw_rows)
         load_k(1, 2)
         load_k(1, 3)
         nc.sync.dma_start(p1_t[:], p1)
@@ -86,46 +77,47 @@ def tile_picked_dynk8_none_p_kernel(
             nc.vector.tensor_copy(k_got[s][t][:], k_win[s][t][:].indirect(cls_t[:]))
 
         gather_k(0, 0, "k00")
+        gather_k(0, 1, "k01")
         xs_got = keep.tile([P, S], U8, name="xs_got", align_bytes=64)
         nc.vector.tensor_copy(xs_got[:], xs_win[:].indirect(offs_t[:]))
         for r in range(4):
             nc.scalar.dma_start(out=xq_scales[r:P:32, :].bitcast(I32), in_=xs_got[8 * r : P : 32, :].bitcast(I32))
-        gather_k(0, 1, "k01")
         gather_k(0, 2, "k02")
         gather_k(0, 3, "k03")
-        xq_words = keep.tile([P, S], U32, name="xq_words", align_bytes=64)
-        nc.vector.tensor_copy(xq_words[:], xw_win[:].indirect(offs_t[:]))
         gather_k(1, 0, "k10")
         gather_k(1, 1, "k11")
 
-        w1_bf = [keep.tile([P, 2, P, 4], BF16, name=f"w1_bf{u}", tag=f"w1_bf{u}", align_bytes=64) for u in range(2)]
-        for h in range(2):
-            for u in range(2):
-                nc.scalar.copy(
-                    out=w1_bf[u][:, :, 64 * h : 64 * (h + 1), :].rearrange("p t (g f) j -> p t g j f", f=4),
-                    in_=w1_raw[h][:].rearrange("p j (g t f) -> p t g j f", t=4, f=4)[:, 2 * u : 2 * u + 2],
-                )
-        y_win = [keep.tile([P, S], F32, name=f"y_win{t}") for t in range(4)]
+        w1_codes, w1_scales = [], []
         for u in range(2):
-            w1_codes = keep.tile([P, 2 * P], U32, name=f"w1_codes{u}", align_bytes=64)
-            w1_scales = keep.tile([P, 2 * P], U8, name=f"w1_scales{u}", align_bytes=64)
-            nc.vector.quantize_mx(
-                out=w1_codes[:].bitcast(FP8X4), scales=w1_scales[:], in_=w1_bf[u][:].rearrange("p t m j -> p (t m j)")
+            w1_bf = keep.tile([P, 2, P, 4], BF16, name=f"w1_bf{u}", align_bytes=64)
+            nc.scalar.copy(
+                out=w1_bf[:].rearrange("p t (g f) j -> p t g j f", f=4),
+                in_=w1_raw[:].rearrange("p j (g t f) -> p t g j f", t=4, f=4)[:, 2 * u : 2 * u + 2],
             )
-            for e in range(2):
-                t = 2 * u + e
-                bank = psum.tile([P, S], F32, name=f"ybank{t}", tag=f"bank{t}")
-                nc.tensor.matmul_mx(
-                    out=bank[:],
-                    lhsT=w1_codes[:, P * e : P * (e + 1)].bitcast(FP8X4),
-                    lhsT_scale=w1_scales[:, P * e : P * (e + 1)],
-                    rhs=xq_words[:].bitcast(FP8X4),
-                    rhs_scale=xq_scales[:],
-                    start=True,
-                    stop=True,
-                )
-                nc.scalar.copy(out=y_win[t][:], in_=bank[:])
-            gather_k(1, 2 + u, f"w1_bf{u}")
+            w1_codes.append(keep.tile([P, 2 * P], U32, name=f"w1_codes{u}", align_bytes=64))
+            w1_scales.append(keep.tile([P, 2 * P], U8, name=f"w1_scales{u}", align_bytes=64))
+            nc.vector.quantize_mx(
+                out=w1_codes[u][:].bitcast(FP8X4), scales=w1_scales[u][:], in_=w1_bf[:].rearrange("p t m j -> p (t m j)")
+            )
+        xq_words = keep.tile([P, S], U32, name="xq_words", align_bytes=64)
+        nc.vector.tensor_copy(xq_words[:], xw_win[:].indirect(offs_t[:]))
+        gather_k(1, 2, "k12")
+        gather_k(1, 3, "k13")
+
+        y_win = [keep.tile([P, 2 * S if t < 2 else S], F32, name=f"y_win{t}") for t in range(4)]
+        for t in range(4):
+            u, e = divmod(t, 2)
+            bank = psum.tile([P, S], F32, name=f"ybank{t}", tag=f"bank{t}")
+            nc.tensor.matmul_mx(
+                out=bank[:],
+                lhsT=w1_codes[u][:, P * e : P * (e + 1)].bitcast(FP8X4),
+                lhsT_scale=w1_scales[u][:, P * e : P * (e + 1)],
+                rhs=xq_words[:].bitcast(FP8X4),
+                rhs_scale=xq_scales[:],
+                start=True,
+                stop=True,
+            )
+            nc.scalar.copy(out=y_win[t][:, 0:S], in_=bank[:])
 
         w2_bf = keep.tile([P, N, 4], BF16, name="w2_bf", align_bytes=64)
         nc.scalar.copy(
@@ -145,36 +137,58 @@ def tile_picked_dynk8_none_p_kernel(
             psum.tile([P, 2, 256], F32, name="back0", tag="bank7"),
             psum.tile([P, 2, 128], F32, name="back1", tag="bank3"),
         ]
-        for t in range(4):
+        prods = keep.tile([P, 8 * S], F32, name="prods", align_bytes=64)
+
+        def row(s, t):
+            return prods[:, S * (2 * t + s) : S * (2 * t + s + 1)]
+
+        def stretch(t, a, n):
             for s in range(2):
-                prod = keep.tile([P, EARLY], F32, name=f"early{s}_{t}", tag=f"early{s}_{t}", align_bytes=64)
-                product(prod[:], s, t, 0, EARLY)
-                for jb in range(3):
+                if n == S:
+                    dst = row(s, t)
+                else:
+                    dst = keep.tile([P, n], F32, name=f"part{a}_{s}_{t}", tag=f"part{a}_{s}_{t}", align_bytes=64)[:]
+                product(dst, s, t, a, n)
+                for jb in range(a // P, min((a + n) // P, 3)):
                     nc.tensor.matmul(
-                        sums[t // 2][jb][:, t % 2, :], prod[:, P * jb : P * (jb + 1)], ident[:],
+                        sums[t // 2][jb][:, t % 2, :], dst[:, P * jb - a : P * (jb + 1) - a], ident[:],
                         start=(s == 0), stop=(s == 1), is_transpose=True,
                     )
-            if t % 2 == 1:
-                u = t // 2
-                for jb in range(3):
-                    turned = keep.tile([P, P, 2], BF16, name=f"turned{jb}_{u}")
-                    nc.scalar.copy(turned[:], sums[u][jb][:].rearrange("j e p -> j p e"))
-                    nc.tensor.transpose(
-                        back[jb // 2][:, u, P * (jb % 2) : P * (jb % 2 + 1)],
-                        turned[:].rearrange("j p e -> j (p e)").bitcast(F32),
-                        ident[:],
-                    )
 
-        w2_codes = keep.tile([P, N], U32, name="w2_codes", tag="early0_3", align_bytes=64)
+        def turn_back(u, blocks):
+            for jb in blocks:
+                turned = keep.tile([P, P, 2], BF16, name=f"turned{jb}_{u}")
+                nc.scalar.copy(turned[:], sums[u][jb][:].rearrange("j e p -> j p e"))
+                nc.tensor.transpose(
+                    back[jb // 2][:, u, P * (jb % 2) : P * (jb % 2 + 1)],
+                    turned[:].rearrange("j p e -> j (p e)").bitcast(F32),
+                    ident[:],
+                )
+
+        out_rows = out.rearrange("(mt p) j -> p mt j", p=P)
+
+        stretch(0, 0, S)
+        stretch(1, 0, S)
+        turn_back(0, range(3))
+        stretch(2, 0, 256)
+        stretch(3, 0, 256)
+        turn_back(1, range(2))
+        z_a = row(1, 2)
+        nc.scalar.copy(z_a.rearrange("p (n u) -> p n u", u=2), back[0][:].rearrange("p u n -> p n u"))
+        stretch(2, 256, P)
+        stretch(3, 256, P)
+        turn_back(1, [2])
+        z_b = keep.tile([P, 256], F32, name="z_b", tag="z_b", align_bytes=64)
+        nc.scalar.copy(z_b[:].rearrange("p (n u) -> p n u", u=2), back[1][:].rearrange("p u n -> p n u"))
+
+        w2_codes = keep.tile([P, N], U32, name="w2_codes", tag="part256_0_3", align_bytes=64)
         w2_scales = keep.tile([P, N], U8, name="w2_scales", align_bytes=64)
         nc.vector.quantize_mx(
             out=w2_codes[:].bitcast(FP8X4), scales=w2_scales[:], in_=w2_bf[:].rearrange("p n j -> p (n j)")
         )
 
-        out_rows = out.rearrange("(mt p) j -> p mt j", p=P)
-
-        def finish(z_bf, a, m, per_bank, bank0, copies, queues):
-            z_codes = keep.tile([P, m], U32, name=f"z_codes{a}", align_bytes=64)
+        def finish(z_bf, a, m, per_bank, bank0, copies, queues, tag):
+            z_codes = keep.tile([P, m], U32, name=f"z_codes{a}", tag=tag, align_bytes=64)
             z_scales = keep.tile([P, m], U8, name=f"z_scales{a}", align_bytes=64)
             nc.vector.quantize_mx(out=z_codes[:].bitcast(FP8X4), scales=z_scales[:], in_=z_bf)
             for g in range(4 // per_bank):
@@ -194,24 +208,16 @@ def tile_picked_dynk8_none_p_kernel(
                 copies[g](res[:], acc[:])
                 queues[g].dma_start(out=out_rows[:, per_bank * g : per_bank * (g + 1), a : a + m], in_=res[:])
 
-        z_a = keep.tile([P, 512], F32, name="z_a", tag="z_a", align_bytes=64)
-        z_b = keep.tile([P, 256], F32, name="z_b", align_bytes=64)
-        nc.scalar.copy(z_a[:].rearrange("p (n u) -> p n u", u=2), back[0][:].rearrange("p u n -> p n u"))
-        nc.scalar.copy(z_b[:].rearrange("p (n u) -> p n u", u=2), back[1][:].rearrange("p u n -> p n u"))
-        planes = keep.tile([P, 4, LATE], BF16, name="planes")
-        for t in range(4):
-            if t == 3:
-                finish(z_a[:].bitcast(BF16), 0, 256, 2, 4, [nc.scalar.copy] * 2, [nc.sync] * 2)
-                finish(z_b[:].bitcast(BF16), 256, 128, 4, 6, [nc.scalar.copy], [nc.sync])
-            late = keep.tile([P, 2, LATE], F32, name=f"late{t}", tag="z_a" if t == 3 else f"late{t}", align_bytes=64)
+        for t in (2, 3):
             for s in range(2):
-                product(late[:, s, :], s, t, EARLY, LATE)
-            nc.vector.tensor_tensor(planes[:, t, :], late[:, 0, :], late[:, 1, :], ADD)
-        z_c = keep.tile([P, LATE, 4], BF16, name="z_c", align_bytes=64)
-        nc.vector.tensor_copy(
-            z_c[:].rearrange("p (c i) t -> p c t i", i=4), planes[:].rearrange("p t (c i) -> p c t i", i=4)
-        )
+                if (t, s) == (2, 1):
+                    finish(z_a.bitcast(BF16), 0, 256, 2, 4, [nc.scalar.copy] * 2, [nc.sync] * 2, "z_codes0")
+                product(row(s, t)[:, EARLY:S], s, t, EARLY, LATE)
+        finish(z_b[:].bitcast(BF16), 256, 128, 4, 6, [nc.scalar.copy], [nc.sync], "k13")
+        z_c = keep.tile([P, LATE, 4], BF16, name="z_c", tag="z_b", align_bytes=64)
+        taps = prods[:].rearrange("p (t s b c i) -> p s b c t i", t=4, s=2, b=4, i=4)
+        nc.vector.tensor_tensor(z_c[:].rearrange("p (c i) t -> p c t i", i=4), taps[:, 0, 3], taps[:, 1, 3], ADD)
         finish(
             z_c[:].rearrange("p n t -> p (n t)"), EARLY, LATE, 1, 0,
-            [nc.scalar.copy, nc.vector.tensor_copy] * 2, [nc.sync, nc.sync, nc.scalar, nc.sync],
+            [nc.scalar.copy, nc.vector.tensor_copy] * 2, [nc.sync, nc.sync, nc.scalar, nc.sync], "z_codes2",
         )

@@ -41,7 +41,7 @@ def tile_picked_dynk8_none_p_kernel(
         xw_rows = x_words[0].rearrange("p n t -> p (n t)").bitcast(I32)
         w1_raw = keep.tile([P, 4, H], F32, name="w1_raw")
         w1_rows = w1.rearrange("(p j) c -> p j c", j=4)
-        w2_raw = keep.tile([P, 4, N], F32, name="w2_raw")
+        w2_raw = keep.tile([P, 4, N], F32, name="w2_raw", tag="w2_raw")
         w2_rows = w2.rearrange("(g t f) u -> t g f u", t=4, f=4)
         xq_scales = keep.tile([P, S], U8, name="xq_scales", align_bytes=64)
         ident = keep.tile([P, P], F32, name="ident")
@@ -104,7 +104,7 @@ def tile_picked_dynk8_none_p_kernel(
         gather_k(1, 2, "k12")
         gather_k(1, 3, "k13")
 
-        y_win = [keep.tile([P, 2 * S if t < 2 else S], F32, name=f"y_win{t}") for t in range(4)]
+        y_win = [keep.tile([P, 2 * S if t == 0 else S], F32, name=f"y_win{t}") for t in range(4)]
         for t in range(4):
             u, e = divmod(t, 2)
             bank = psum.tile([P, S], F32, name=f"ybank{t}", tag=f"bank{t}")
@@ -130,22 +130,17 @@ def tile_picked_dynk8_none_p_kernel(
             nc.vector.tensor_tensor(dst, y_win[t][:].indirect(places), k_got[s][t][:, a : a + n], MULT)
 
         sums = [
-            [psum.tile([P, 2, P], F32, name=f"sums{u}_{jb}", tag=f"bank{4 * (1 - u) + jb}") for jb in range(3)]
+            [psum.tile([P, 2, P], F32, name=f"sums{u}_{jb}", tag=f"bank{6 - jb if u else 4 + jb}") for jb in range(3 - u)]
             for u in range(2)
         ]
-        back = [
-            psum.tile([P, 2, 256], F32, name="back0", tag="bank7"),
-            psum.tile([P, 2, 128], F32, name="back1", tag="bank3"),
-        ]
-        prods = keep.tile([P, 8 * S], F32, name="prods", align_bytes=64)
-
-        def row(s, t):
-            return prods[:, S * (2 * t + s) : S * (2 * t + s + 1)]
+        back = [psum.tile([P, 2, P], F32, name=f"back{jb}", tag=f"bank{(7, 2, 3)[jb]}") for jb in range(3)]
+        ROW = EARLY + 4 * LATE
+        prods = keep.tile([P, 2 * ROW], F32, name="prods", align_bytes=64)
 
         def stretch(t, a, n):
             for s in range(2):
                 if n == S:
-                    dst = row(s, t)
+                    dst = prods[:, ROW * s : ROW * s + S]
                 else:
                     dst = keep.tile([P, n], F32, name=f"part{a}_{s}_{t}", tag=f"part{a}_{s}_{t}", align_bytes=64)[:]
                 product(dst, s, t, a, n)
@@ -155,44 +150,50 @@ def tile_picked_dynk8_none_p_kernel(
                         start=(s == 0), stop=(s == 1), is_transpose=True,
                     )
 
-        def turn_back(u, blocks):
-            for jb in blocks:
-                turned = keep.tile([P, P, 2], BF16, name=f"turned{jb}_{u}")
-                nc.scalar.copy(turned[:], sums[u][jb][:].rearrange("j e p -> j p e"))
-                nc.tensor.transpose(
-                    back[jb // 2][:, u, P * (jb % 2) : P * (jb % 2 + 1)],
-                    turned[:].rearrange("j p e -> j (p e)").bitcast(F32),
-                    ident[:],
-                )
+        def turn_back(u, blocks, tag):
+            turned = keep.tile([P, 2 * P * len(blocks)], BF16, name=f"turned{u}_{blocks[0]}", tag=tag)
+            for b, jb in enumerate(blocks):
+                pairs = turned[:, 2 * P * b : 2 * P * (b + 1)]
+                nc.scalar.copy(pairs.rearrange("j (p e) -> j p e", e=2), sums[u][jb][:].rearrange("j e p -> j p e"))
+                nc.tensor.transpose(back[jb][:, u, :], pairs.bitcast(F32), ident[:])
+
+        def weave(dst, jb):
+            nc.scalar.copy(dst.rearrange("p (n u) -> p n u", u=2), back[jb][:].rearrange("p u n -> p n u"))
 
         out_rows = out.rearrange("(mt p) j -> p mt j", p=P)
 
         stretch(0, 0, S)
-        stretch(1, 0, S)
-        turn_back(0, range(3))
+        stretch(1, 0, EARLY)
+        turn_back(0, range(3), "w2_raw")
         stretch(2, 0, 256)
         stretch(3, 0, 256)
-        turn_back(1, range(2))
-        z_a = row(1, 2)
-        nc.scalar.copy(z_a.rearrange("p (n u) -> p n u", u=2), back[0][:].rearrange("p u n -> p n u"))
+        turn_back(1, range(2), "w2_raw")
+        z_a = [prods[:, ROW - 256 : ROW], prods[:, 2 * ROW - 320 : 2 * ROW - 64]]
+        weave(z_a[0], 0)
+        weave(z_a[1], 1)
+        sums[1].append(psum.tile([P, 2, P], F32, name="sums1_2", tag="bank5"))
         stretch(2, 256, P)
         stretch(3, 256, P)
-        turn_back(1, [2])
+        turn_back(1, [2], "w2_raw")
         z_b = keep.tile([P, 256], F32, name="z_b", tag="z_b", align_bytes=64)
-        nc.scalar.copy(z_b[:].rearrange("p (n u) -> p n u", u=2), back[1][:].rearrange("p u n -> p n u"))
+        weave(z_b[:], 2)
 
-        w2_codes = keep.tile([P, N], U32, name="w2_codes", tag="part256_0_3", align_bytes=64)
+        w2_codes = keep.tile([P, N], U32, name="w2_codes", tag="part0_1_3", align_bytes=64)
         w2_scales = keep.tile([P, N], U8, name="w2_scales", align_bytes=64)
         nc.vector.quantize_mx(
             out=w2_codes[:].bitcast(FP8X4), scales=w2_scales[:], in_=w2_bf[:].rearrange("p n j -> p (n j)")
         )
 
-        def finish(z_bf, a, m, per_bank, bank0, copies, queues, tag):
+        def finish(blocks, a, banks, copies, queues, tag):
+            m = P * len(blocks)
+            per_bank = 4 // len(banks)
             z_codes = keep.tile([P, m], U32, name=f"z_codes{a}", tag=tag, align_bytes=64)
             z_scales = keep.tile([P, m], U8, name=f"z_scales{a}", align_bytes=64)
-            nc.vector.quantize_mx(out=z_codes[:].bitcast(FP8X4), scales=z_scales[:], in_=z_bf)
-            for g in range(4 // per_bank):
-                acc = psum.tile([P, per_bank, m], F32, name=f"acc{a}_{g}", tag=f"bank{bank0 + g}")
+            for b, z_bf in enumerate(blocks):
+                cols = slice(P * b, P * (b + 1))
+                nc.vector.quantize_mx(out=z_codes[:, cols].bitcast(FP8X4), scales=z_scales[:, cols], in_=z_bf)
+            for g, bank in enumerate(banks):
+                acc = psum.tile([P, per_bank, m], F32, name=f"acc{a}_{g}", tag=f"bank{bank}")
                 res = keep.tile([P, per_bank, m], F32, name=f"res{a}_{g}")
                 for q in range(per_bank):
                     mt = per_bank * g + q
@@ -208,16 +209,16 @@ def tile_picked_dynk8_none_p_kernel(
                 copies[g](res[:], acc[:])
                 queues[g].dma_start(out=out_rows[:, per_bank * g : per_bank * (g + 1), a : a + m], in_=res[:])
 
-        for t in (2, 3):
+        for t in (1, 2, 3):
             for s in range(2):
-                if (t, s) == (2, 1):
-                    finish(z_a.bitcast(BF16), 0, 256, 2, 4, [nc.scalar.copy] * 2, [nc.sync] * 2, "z_codes0")
-                product(row(s, t)[:, EARLY:S], s, t, EARLY, LATE)
-        finish(z_b[:].bitcast(BF16), 256, 128, 4, 6, [nc.scalar.copy], [nc.sync], "k13")
+                if (t, s) == (1, 1):
+                    finish([z.bitcast(BF16) for z in z_a], 0, (5, 3), [nc.scalar.copy] * 2, [nc.sync] * 2, "z_codes0")
+                product(prods[:, ROW * s + EARLY + LATE * t : ROW * s + EARLY + LATE * (t + 1)], s, t, EARLY, LATE)
+        finish([z_b[:].bitcast(BF16)], 256, (6, 7), [nc.scalar.copy] * 2, [nc.sync] * 2, "k13")
         z_c = keep.tile([P, LATE, 4], BF16, name="z_c", tag="z_b", align_bytes=64)
-        taps = prods[:].rearrange("p (t s b c i) -> p s b c t i", t=4, s=2, b=4, i=4)
-        nc.vector.tensor_tensor(z_c[:].rearrange("p (c i) t -> p c t i", i=4), taps[:, 0, 3], taps[:, 1, 3], ADD)
+        taps = [prods[:, ROW * s + EARLY : ROW * (s + 1)].rearrange("p (t c i) -> p c t i", t=4, i=4) for s in range(2)]
+        nc.vector.tensor_tensor(z_c[:].rearrange("p (c i) t -> p c t i", i=4), taps[0], taps[1], ADD)
         finish(
-            z_c[:].rearrange("p n t -> p (n t)"), EARLY, LATE, 1, 0,
+            [z_c[:].rearrange("p n t -> p (n t)")], EARLY, (0, 1, 2, 4),
             [nc.scalar.copy, nc.vector.tensor_copy] * 2, [nc.sync, nc.sync, nc.scalar, nc.sync], "z_codes2",
         )

@@ -52,8 +52,8 @@ def tile_picked_dynk8_none_p_kernel(
         def load_k(s, t):
             nc.sync.dma_start(out=k_win[s][t][:, 0:U], in_=k_rows[s][t])
 
-        nc.sync.dma_start(cls_t[:], cls)
         load_k(0, 0)
+        nc.sync.dma_start(cls_t[:], cls)
         nc.sync.dma_start(offs_t[:], offs)
         load_k(0, 1)
         nc.sync.dma_start(out=xs_win[0:P:8, :].bitcast(I32), in_=x_scales[0].bitcast(I32))
@@ -168,7 +168,7 @@ def tile_picked_dynk8_none_p_kernel(
         stretch(2, 0, 256)
         stretch(3, 0, 256)
         turn_back(1, range(2), "w2_raw")
-        z_a = [prods[:, ROW - 256 : ROW], prods[:, 2 * ROW - 320 : 2 * ROW - 64]]
+        z_a = [prods[:, ROW - 256 : ROW], prods[:, 2 * ROW - 256 : 2 * ROW]]
         weave(z_a[0], 0)
         weave(z_a[1], 1)
         sums[1].append(psum.tile([P, 2, P], F32, name="sums1_2", tag="bank5"))
@@ -211,7 +211,7 @@ def tile_picked_dynk8_none_p_kernel(
 
         for t in (1, 2, 3):
             for s in range(2):
-                if (t, s) == (1, 1):
+                if (t, s) == (2, 0):
                     finish([z.bitcast(BF16) for z in z_a], 0, (5, 3), [nc.scalar.copy] * 2, [nc.sync] * 2, "z_codes0")
                 product(prods[:, ROW * s + EARLY + LATE * t : ROW * s + EARLY + LATE * (t + 1)], s, t, EARLY, LATE)
         finish([z_b[:].bitcast(BF16)], 256, (6, 7), [nc.scalar.copy] * 2, [nc.sync] * 2, "k13")
@@ -220,5 +220,5 @@ def tile_picked_dynk8_none_p_kernel(
         nc.vector.tensor_tensor(z_c[:].rearrange("p (c i) t -> p c t i", i=4), taps[0], taps[1], ADD)
         finish(
             [z_c[:].rearrange("p n t -> p (n t)")], EARLY, (0, 1, 2, 4),
-            [nc.scalar.copy, nc.vector.tensor_copy] * 2, [nc.sync, nc.sync, nc.scalar, nc.sync], "z_codes2",
+            [nc.vector.tensor_copy, nc.scalar.copy] * 2, [nc.sync, nc.sync, nc.sync, nc.scalar], "z_codes2",
         )

@@ -150,8 +150,7 @@ def tile_picked_dynk8_none_p_kernel(
                         start=(s == 0), stop=(s == 1), is_transpose=True,
                     )
 
-        def turn_back(u, blocks, tag):
-            turned = keep.tile([P, 2 * P * len(blocks)], BF16, name=f"turned{u}_{blocks[0]}", tag=tag)
+        def turn_back(u, blocks, turned):
             for b, jb in enumerate(blocks):
                 pairs = turned[:, 2 * P * b : 2 * P * (b + 1)]
                 nc.scalar.copy(pairs.rearrange("j (p e) -> j p e", e=2), sums[u][jb][:].rearrange("j e p -> j p e"))
@@ -164,18 +163,18 @@ def tile_picked_dynk8_none_p_kernel(
 
         stretch(0, 0, S)
         stretch(1, 0, EARLY)
-        turn_back(0, range(3), "w2_raw")
+        turn_back(0, range(3), keep.tile([P, 6 * P], BF16, name="turned0", tag="w2_raw"))
         stretch(2, 0, 256)
         stretch(3, 0, 256)
-        turn_back(1, range(2), "w2_raw")
-        z_a = [prods[:, ROW - 256 : ROW], prods[:, 2 * ROW - 256 : 2 * ROW]]
+        turn_back(1, range(2), keep.tile([P, 4 * P], BF16, name="turned1", tag="w2_raw"))
+        z_a = [prods[:, ROW - 256 : ROW], keep.tile([P, 256], F32, name="z_a1", align_bytes=64)[:]]
         weave(z_a[0], 0)
         weave(z_a[1], 1)
         sums[1].append(psum.tile([P, 2, P], F32, name="sums1_2", tag="bank5"))
         stretch(2, 256, P)
         stretch(3, 256, P)
-        turn_back(1, [2], "w2_raw")
-        z_b = keep.tile([P, 256], F32, name="z_b", tag="z_b", align_bytes=64)
+        turn_back(1, [2], prods[:, 2 * ROW - 192 : 2 * ROW - 64].bitcast(BF16))
+        z_b = keep.tile([P, 256], F32, name="z_b", align_bytes=64)
         weave(z_b[:], 2)
 
         w2_codes = keep.tile([P, N], U32, name="w2_codes", tag="part0_1_3", align_bytes=64)
@@ -209,13 +208,17 @@ def tile_picked_dynk8_none_p_kernel(
                 copies[g](res[:], acc[:])
                 queues[g].dma_start(out=out_rows[:, per_bank * g : per_bank * (g + 1), a : a + m], in_=res[:])
 
-        for t in (1, 2, 3):
-            for s in range(2):
-                if (t, s) == (2, 0):
-                    finish([z.bitcast(BF16) for z in z_a], 0, (5, 3), [nc.scalar.copy] * 2, [nc.sync] * 2, "z_codes0")
-                product(prods[:, ROW * s + EARLY + LATE * t : ROW * s + EARLY + LATE * (t + 1)], s, t, EARLY, LATE)
-        finish([z_b[:].bitcast(BF16)], 256, (6, 7), [nc.scalar.copy] * 2, [nc.sync] * 2, "k13")
-        z_c = keep.tile([P, LATE, 4], BF16, name="z_c", tag="z_b", align_bytes=64)
+        def late_product(s, t):
+            product(prods[:, ROW * s + EARLY + LATE * t : ROW * s + EARLY + LATE * (t + 1)], s, t, EARLY, LATE)
+
+        late_product(0, 1)
+        late_product(1, 1)
+        finish([z.bitcast(BF16) for z in z_a], 0, (5, 3), [nc.scalar.copy] * 2, [nc.sync] * 2, "z_codes0")
+        for s in range(2):
+            for t in (2, 3):
+                late_product(s, t)
+        finish([z_b[:].bitcast(BF16)], 256, (6, 7), [nc.scalar.copy] * 2, [nc.sync] * 2, "z_codes1")
+        z_c = keep.tile([P, LATE, 4], BF16, name="z_c", align_bytes=64)
         taps = [prods[:, ROW * s + EARLY : ROW * (s + 1)].rearrange("p (t c i) -> p c t i", t=4, i=4) for s in range(2)]
         nc.vector.tensor_tensor(z_c[:].rearrange("p (c i) t -> p c t i", i=4), taps[0], taps[1], ADD)
         finish(

@@ -141,6 +141,8 @@ def tile_picked_dynk8_none_p_kernel(
             for s in range(2):
                 if n == S:
                     dst = prods[:, ROW * s : ROW * s + S]
+                elif (a, s, t) == (256, 1, 2):
+                    dst = prods[:, ROW + S : ROW + S + LATE]
                 else:
                     dst = keep.tile([P, n], F32, name=f"part{a}_{s}_{t}", tag=f"part{a}_{s}_{t}", align_bytes=64)[:]
                 product(dst, s, t, a, n)
@@ -183,12 +185,14 @@ def tile_picked_dynk8_none_p_kernel(
             out=w2_codes[:].bitcast(FP8X4), scales=w2_scales[:], in_=w2_bf[:].rearrange("p n j -> p (n j)")
         )
 
-        def finish(blocks, a, banks, copies, queues, tag):
+        def finish(blocks, a, banks, copies, queues, tag, between=None):
             m = P * len(blocks)
             per_bank = 4 // len(banks)
             z_codes = keep.tile([P, m], U32, name=f"z_codes{a}", tag=tag, align_bytes=64)
             z_scales = keep.tile([P, m], U8, name=f"z_scales{a}", align_bytes=64)
             for b, z_bf in enumerate(blocks):
+                if b:
+                    between()
                 cols = slice(P * b, P * (b + 1))
                 nc.vector.quantize_mx(out=z_codes[:, cols].bitcast(FP8X4), scales=z_scales[:, cols], in_=z_bf)
             for g, bank in enumerate(banks):
@@ -212,8 +216,7 @@ def tile_picked_dynk8_none_p_kernel(
             product(prods[:, ROW * s + EARLY + LATE * t : ROW * s + EARLY + LATE * (t + 1)], s, t, EARLY, LATE)
 
         late_product(0, 1)
-        late_product(1, 1)
-        finish([z.bitcast(BF16) for z in z_a], 0, (5, 3), [nc.scalar.copy] * 2, [nc.sync] * 2, "z_codes0")
+        finish([z.bitcast(BF16) for z in z_a], 0, (5, 3), [nc.scalar.copy] * 2, [nc.sync] * 2, "z_codes0", lambda: late_product(1, 1))
         for s in range(2):
             for t in (2, 3):
                 late_product(s, t)

@@ -130,7 +130,7 @@ def tile_picked_dynk8_none_p_kernel(
             nc.vector.tensor_tensor(dst, y_win[t][:].indirect(places), k_got[s][t][:, a : a + n], MULT)
 
         sums = [
-            [psum.tile([P, 2, P], F32, name=f"sums{u}_{jb}", tag=f"bank{6 - jb if u else 4 + jb}") for jb in range(3 - u)]
+            [psum.tile([P, 2, P], F32, name=f"sums{u}_{jb}", tag=f"bank{4 + jb}") for jb in range(3)]
             for u in range(2)
         ]
         back = [psum.tile([P, 2, P], F32, name=f"back{jb}", tag=f"bank{(7, 2, 3)[jb]}") for jb in range(3)]
@@ -141,8 +141,10 @@ def tile_picked_dynk8_none_p_kernel(
             for s in range(2):
                 if n == S:
                     dst = prods[:, ROW * s : ROW * s + S]
-                elif (a, s, t) == (256, 1, 2):
-                    dst = prods[:, ROW + S : ROW + S + LATE]
+                elif (t, a) == (3, 0):
+                    dst = prods[:, (ROW + LATE) * s + S : (ROW + LATE) * s + S + n]
+                elif (t, a, s) == (3, 256, 0):
+                    dst = prods[:, ROW + S : ROW + S + n]
                 else:
                     dst = keep.tile([P, n], F32, name=f"part{a}_{s}_{t}", tag=f"part{a}_{s}_{t}", align_bytes=64)[:]
                 product(dst, s, t, a, n)
@@ -166,33 +168,28 @@ def tile_picked_dynk8_none_p_kernel(
         stretch(0, 0, S)
         stretch(1, 0, EARLY)
         turn_back(0, range(3), keep.tile([P, 6 * P], BF16, name="turned0", tag="w2_raw"))
-        stretch(2, 0, 256)
+        stretch(2, 0, EARLY)
         stretch(3, 0, 256)
-        turn_back(1, range(2), keep.tile([P, 4 * P], BF16, name="turned1", tag="w2_raw"))
+        stretch(3, 256, P)
+        turn_back(1, range(3), keep.tile([P, 6 * P], BF16, name="turned1", tag="w2_raw"))
         z_a = [prods[:, ROW - 256 : ROW], keep.tile([P, 256], F32, name="z_a1", align_bytes=64)[:]]
         weave(z_a[0], 0)
         weave(z_a[1], 1)
-        sums[1].append(psum.tile([P, 2, P], F32, name="sums1_2", tag="bank5"))
-        stretch(2, 256, P)
-        stretch(3, 256, P)
-        turn_back(1, [2], prods[:, 2 * ROW - 192 : 2 * ROW - 64].bitcast(BF16))
         z_b = keep.tile([P, 256], F32, name="z_b", align_bytes=64)
         weave(z_b[:], 2)
 
-        w2_codes = keep.tile([P, N], U32, name="w2_codes", tag="part0_1_3", align_bytes=64)
+        w2_codes = keep.tile([P, N], U32, name="w2_codes", tag="part0_1_2", align_bytes=64)
         w2_scales = keep.tile([P, N], U8, name="w2_scales", align_bytes=64)
         nc.vector.quantize_mx(
             out=w2_codes[:].bitcast(FP8X4), scales=w2_scales[:], in_=w2_bf[:].rearrange("p n j -> p (n j)")
         )
 
-        def finish(blocks, a, banks, copies, queues, tag, between=None):
+        def finish(blocks, a, banks, copies, queues, tag):
             m = P * len(blocks)
             per_bank = 4 // len(banks)
             z_codes = keep.tile([P, m], U32, name=f"z_codes{a}", tag=tag, align_bytes=64)
             z_scales = keep.tile([P, m], U8, name=f"z_scales{a}", align_bytes=64)
             for b, z_bf in enumerate(blocks):
-                if b:
-                    between()
                 cols = slice(P * b, P * (b + 1))
                 nc.vector.quantize_mx(out=z_codes[:, cols].bitcast(FP8X4), scales=z_scales[:, cols], in_=z_bf)
             for g, bank in enumerate(banks):
@@ -215,16 +212,16 @@ def tile_picked_dynk8_none_p_kernel(
         def late_product(s, t):
             product(prods[:, ROW * s + EARLY + LATE * t : ROW * s + EARLY + LATE * (t + 1)], s, t, EARLY, LATE)
 
-        late_product(0, 1)
-        finish([z.bitcast(BF16) for z in z_a], 0, (5, 3), [nc.scalar.copy] * 2, [nc.sync] * 2, "z_codes0", lambda: late_product(1, 1))
-        for s in range(2):
-            for t in (2, 3):
-                late_product(s, t)
-        finish([z_b[:].bitcast(BF16)], 256, (6, 7), [nc.scalar.copy] * 2, [nc.sync] * 2, "z_codes1")
+        for s, t in ((0, 1), (1, 1), (1, 2), (1, 3)):
+            late_product(s, t)
+        finish([z.bitcast(BF16) for z in z_a], 0, (0, 1, 4, 5), [nc.scalar.copy] * 4, [nc.sync] * 4, "z_codes0")
+        late_product(0, 2)
+        late_product(0, 3)
+        finish([z_b[:].bitcast(BF16)], 256, (6,), [nc.scalar.copy], [nc.scalar], "k02")
         z_c = keep.tile([P, LATE, 4], BF16, name="z_c", align_bytes=64)
         taps = [prods[:, ROW * s + EARLY : ROW * (s + 1)].rearrange("p (t c i) -> p c t i", t=4, i=4) for s in range(2)]
         nc.vector.tensor_tensor(z_c[:].rearrange("p (c i) t -> p c t i", i=4), taps[0], taps[1], ADD)
         finish(
-            [z_c[:].rearrange("p n t -> p (n t)")], EARLY, (0, 1, 2, 4),
-            [nc.vector.tensor_copy, nc.scalar.copy] * 2, [nc.sync, nc.sync, nc.sync, nc.scalar], "z_codes2",
+            [z_c[:].rearrange("p n t -> p (n t)")], EARLY, (7, 2, 3, 0),
+            [nc.vector.tensor_copy] * 4, [nc.sync] * 4, "z_codes2",
         )

@@ -18,6 +18,7 @@ ADD = mybir.AluOpType.add
 P = 128
 EARLY = 384
 LATE = S - EARLY
+FIRST = 256
 
 
 def tile_picked_dynk8_none_p_kernel(
@@ -52,19 +53,19 @@ def tile_picked_dynk8_none_p_kernel(
         def load_k(s, t):
             nc.sync.dma_start(out=k_win[s][t][:, 0:U], in_=k_rows[s][t])
 
-        load_k(0, 0)
+        load_k(0, 3)
         nc.sync.dma_start(cls_t[:], cls)
         nc.sync.dma_start(offs_t[:], offs)
-        load_k(0, 1)
-        nc.sync.dma_start(out=xs_win[0:P:8, :].bitcast(I32), in_=x_scales[0].bitcast(I32))
         load_k(0, 2)
-        load_k(0, 3)
+        nc.sync.dma_start(out=xs_win[0:P:8, :].bitcast(I32), in_=x_scales[0].bitcast(I32))
+        load_k(0, 1)
+        load_k(0, 0)
         nc.sync.dma_start(out=w1_raw[:], in_=w1_rows)
-        load_k(1, 0)
-        load_k(1, 1)
-        nc.sync.dma_start(out=xw_win[:].bitcast(I32), in_=xw_rows)
-        load_k(1, 2)
         load_k(1, 3)
+        load_k(1, 2)
+        nc.sync.dma_start(out=xw_win[:].bitcast(I32), in_=xw_rows)
+        load_k(1, 1)
+        load_k(1, 0)
         nc.sync.dma_start(p1_t[:], p1)
         nc.sync.dma_start(p2_t[:], p2)
         for t in range(4):
@@ -72,42 +73,42 @@ def tile_picked_dynk8_none_p_kernel(
 
         k_got = [[None] * 4, [None] * 4]
 
-        def gather_k(s, t, tag):
-            k_got[s][t] = keep.tile([P, S], F32, name=f"k_got{s}_{t}", tag=tag, align_bytes=64)
+        def gather_k(s, t):
+            k_got[s][t] = keep.tile([P, S], F32, name=f"k_got{s}_{t}", tag=f"k{s}{t}", align_bytes=64)
             nc.vector.tensor_copy(k_got[s][t][:], k_win[s][t][:].indirect(cls_t[:]))
 
-        gather_k(0, 0, "k00")
-        gather_k(0, 1, "k01")
+        gather_k(0, 3)
+        gather_k(0, 2)
         xs_got = keep.tile([P, S], U8, name="xs_got", align_bytes=64)
         nc.vector.tensor_copy(xs_got[:], xs_win[:].indirect(offs_t[:]))
         for r in range(4):
             nc.scalar.dma_start(out=xq_scales[r:P:32, :].bitcast(I32), in_=xs_got[8 * r : P : 32, :].bitcast(I32))
-        gather_k(0, 2, "k02")
-        gather_k(0, 3, "k03")
-        gather_k(1, 0, "k10")
-        gather_k(1, 1, "k11")
+        gather_k(0, 1)
+        gather_k(0, 0)
+        gather_k(1, 3)
+        gather_k(1, 2)
 
-        w1_codes, w1_scales = [], []
-        for u in range(2):
+        w1_codes, w1_scales = [None] * 2, [None] * 2
+        for u in (1, 0):
             w1_bf = keep.tile([P, 2, P, 4], BF16, name=f"w1_bf{u}", align_bytes=64)
             nc.scalar.copy(
                 out=w1_bf[:].rearrange("p t (g f) j -> p t g j f", f=4),
                 in_=w1_raw[:].rearrange("p j (g t f) -> p t g j f", t=4, f=4)[:, 2 * u : 2 * u + 2],
             )
-            w1_codes.append(keep.tile([P, 2 * P], U32, name=f"w1_codes{u}", align_bytes=64))
-            w1_scales.append(keep.tile([P, 2 * P], U8, name=f"w1_scales{u}", align_bytes=64))
+            w1_codes[u] = keep.tile([P, 2 * P], U32, name=f"w1_codes{u}", align_bytes=64)
+            w1_scales[u] = keep.tile([P, 2 * P], U8, name=f"w1_scales{u}", align_bytes=64)
             nc.vector.quantize_mx(
                 out=w1_codes[u][:].bitcast(FP8X4), scales=w1_scales[u][:], in_=w1_bf[:].rearrange("p t m j -> p (t m j)")
             )
         xq_words = keep.tile([P, S], U32, name="xq_words", align_bytes=64)
         nc.vector.tensor_copy(xq_words[:], xw_win[:].indirect(offs_t[:]))
-        gather_k(1, 2, "k12")
-        gather_k(1, 3, "k13")
+        gather_k(1, 1)
+        gather_k(1, 0)
 
-        y_win = [keep.tile([P, 2 * S if t == 0 else S], F32, name=f"y_win{t}") for t in range(4)]
-        for t in range(4):
+        y_win = [keep.tile([P, 2 * S if t == 3 else S], F32, name=f"y_win{t}") for t in range(4)]
+        for t in (3, 2, 1, 0):
             u, e = divmod(t, 2)
-            bank = psum.tile([P, S], F32, name=f"ybank{t}", tag=f"bank{t}")
+            bank = psum.tile([P, S], F32, name=f"ybank{t}", tag=f"bank{3 - t}")
             nc.tensor.matmul_mx(
                 out=bank[:],
                 lhsT=w1_codes[u][:, P * e : P * (e + 1)].bitcast(FP8X4),
@@ -125,103 +126,115 @@ def tile_picked_dynk8_none_p_kernel(
             in_=w2_raw[:].rearrange("p j (c i) -> p c j i", i=4),
         )
 
+        ROW = P + S
+        prods = keep.tile([P, 2 * ROW], F32, name="prods", align_bytes=64)
+
+        def slot(s, t, n=LATE):
+            return prods[:, ROW * s + P * (t + 1) : ROW * s + P * (t + 1) + n]
+
         def product(dst, s, t, a, n):
             places = (p1_t, p2_t)[s][:, a // 16 : (a + n) // 16]
             nc.vector.tensor_tensor(dst, y_win[t][:].indirect(places), k_got[s][t][:, a : a + n], MULT)
 
-        sums = [
-            [psum.tile([P, 2, P], F32, name=f"sums{u}_{jb}", tag=f"bank{4 + jb}") for jb in range(3)]
-            for u in range(2)
-        ]
-        back = [psum.tile([P, 2, P], F32, name=f"back{jb}", tag=f"bank{(7, 2, 3)[jb]}") for jb in range(3)]
-        ROW = EARLY + 4 * LATE
-        prods = keep.tile([P, 2 * ROW], F32, name="prods", align_bytes=64)
+        sums = {}
+        back = [psum.tile([P, 2, P], F32, name=f"back{jb}", tag=f"bank{(7, 2, 3)[jb]}")[:] for jb in range(3)]
 
-        def stretch(t, a, n):
-            for s in range(2):
-                if n == S:
-                    dst = prods[:, ROW * s : ROW * s + S]
-                elif (t, a) == (3, 0):
-                    dst = prods[:, (ROW + LATE) * s + S : (ROW + LATE) * s + S + n]
-                elif (t, a, s) == (3, 256, 0):
-                    dst = prods[:, ROW + S : ROW + S + n]
-                else:
-                    dst = keep.tile([P, n], F32, name=f"part{a}_{s}_{t}", tag=f"part{a}_{s}_{t}", align_bytes=64)[:]
-                product(dst, s, t, a, n)
-                for jb in range(a // P, min((a + n) // P, 3)):
-                    nc.tensor.matmul(
-                        sums[t // 2][jb][:, t % 2, :], dst[:, P * jb - a : P * (jb + 1) - a], ident[:],
-                        start=(s == 0), stop=(s == 1), is_transpose=True,
-                    )
+        def open_sums(u):
+            for jb in range(3):
+                sums[u, jb] = psum.tile([P, 2, P], F32, name=f"sums{u}_{jb}", tag=f"bank{4 + jb}")[:]
 
-        def turn_back(u, blocks, turned):
-            for b, jb in enumerate(blocks):
-                pairs = turned[:, 2 * P * b : 2 * P * (b + 1)]
-                nc.scalar.copy(pairs.rearrange("j (p e) -> j p e", e=2), sums[u][jb][:].rearrange("j e p -> j p e"))
-                nc.tensor.transpose(back[jb][:, u, :], pairs.bitcast(F32), ident[:])
+        def turn(src, s, t, jb):
+            nc.tensor.matmul(sums[t // 2, jb][:, t % 2, :], src, ident[:], start=(s == 0), stop=(s == 1), is_transpose=True)
+
+        def turn_back(u, jb, pairs):
+            nc.scalar.copy(pairs.rearrange("j (p e) -> j p e", e=2), sums[u, jb].rearrange("j e p -> j p e"))
+            nc.tensor.transpose(back[jb][:, u, :], pairs.bitcast(F32), ident[:])
 
         def weave(dst, jb):
-            nc.scalar.copy(dst.rearrange("p (n u) -> p n u", u=2), back[jb][:].rearrange("p u n -> p n u"))
+            nc.scalar.copy(dst.rearrange("p (n u) -> p n u", u=2), back[jb].rearrange("p u n -> p n u"))
 
-        out_rows = out.rearrange("(mt p) j -> p mt j", p=P)
+        def early(t, a, n, in_slots):
+            for s in range(2):
+                if in_slots:
+                    dst = slot(s, 0, n)
+                else:
+                    dst = keep.tile([P, n], F32, name=f"early{t}_{a}_{s}", align_bytes=64)[:]
+                product(dst, s, t, a, n)
+                for jb in range(a // P, min((a + n) // P, 3)):
+                    turn(dst[:, P * jb - a : P * (jb + 1) - a], s, t, jb)
 
-        stretch(0, 0, S)
-        stretch(1, 0, EARLY)
-        turn_back(0, range(3), keep.tile([P, 6 * P], BF16, name="turned0", tag="w2_raw"))
-        stretch(2, 0, EARLY)
-        stretch(3, 0, 256)
-        stretch(3, 256, P)
-        turn_back(1, range(3), keep.tile([P, 6 * P], BF16, name="turned1", tag="w2_raw"))
-        z_a = [prods[:, ROW - 256 : ROW], keep.tile([P, 256], F32, name="z_a1", align_bytes=64)[:]]
-        weave(z_a[0], 0)
-        weave(z_a[1], 1)
-        z_b = keep.tile([P, 256], F32, name="z_b", align_bytes=64)
+        open_sums(1)
+        early(3, 0, S, True)
+        early(2, 0, EARLY, False)
+        turned = keep.tile([P, 6 * P], BF16, name="turned1", tag="w2_raw")
+        for jb in range(3):
+            turn_back(1, jb, turned[:, 2 * P * jb : 2 * P * (jb + 1)])
+
+        open_sums(0)
+        early(1, 0, EARLY, False)
+        early(0, 0, FIRST, False)
+        early(0, FIRST, P, False)
+        turned = keep.tile([P, 6 * P], BF16, name="turned0", tag="w2_raw")
+        for jb in range(3):
+            turn_back(0, jb, turned[:, 2 * P * jb : 2 * P * (jb + 1)])
+        z_a = [slot(1, 0, 2 * P), slot(0, -1, 2 * P)]
+        for jb in range(2):
+            weave(z_a[jb], jb)
+        z_b = keep.tile([P, 2 * P], F32, name="z_b", align_bytes=64)
         weave(z_b[:], 2)
 
-        w2_codes = keep.tile([P, N], U32, name="w2_codes", tag="part0_1_2", align_bytes=64)
+        def late(s, t):
+            product(slot(s, t), s, t, EARLY, LATE)
+
+        late(0, 2)
+        late(1, 2)
+        late(0, 1)
+        w2_codes = keep.tile([P, N], U32, name="w2_codes", align_bytes=64)
         w2_scales = keep.tile([P, N], U8, name="w2_scales", align_bytes=64)
         nc.vector.quantize_mx(
             out=w2_codes[:].bitcast(FP8X4), scales=w2_scales[:], in_=w2_bf[:].rearrange("p n j -> p (n j)")
         )
+        out_rows = out.rearrange("(mt p) j -> p mt j", p=P)
+        seen = []
 
-        def finish(blocks, a, banks, copies, queues, tag):
+        def quantise(blocks, a, tag):
             m = P * len(blocks)
-            per_bank = 4 // len(banks)
             z_codes = keep.tile([P, m], U32, name=f"z_codes{a}", tag=tag, align_bytes=64)
             z_scales = keep.tile([P, m], U8, name=f"z_scales{a}", align_bytes=64)
             for b, z_bf in enumerate(blocks):
                 cols = slice(P * b, P * (b + 1))
                 nc.vector.quantize_mx(out=z_codes[:, cols].bitcast(FP8X4), scales=z_scales[:, cols], in_=z_bf)
-            for g, bank in enumerate(banks):
-                acc = psum.tile([P, per_bank, m], F32, name=f"acc{a}_{g}", tag=f"bank{bank}")
-                res = keep.tile([P, per_bank, m], F32, name=f"res{a}_{g}")
-                for q in range(per_bank):
-                    mt = per_bank * g + q
-                    nc.tensor.matmul_mx(
-                        out=acc[:, q, :],
-                        lhsT=w2_codes[:, P * mt : P * (mt + 1)].bitcast(FP8X4),
-                        lhsT_scale=w2_scales[:, P * mt : P * (mt + 1)],
-                        rhs=z_codes[:].bitcast(FP8X4),
-                        rhs_scale=z_scales[:],
-                        start=True,
-                        stop=True,
-                    )
-                copies[g](res[:], acc[:])
-                queues[g].dma_start(out=out_rows[:, per_bank * g : per_bank * (g + 1), a : a + m], in_=res[:])
+            return z_codes, z_scales, a, m
 
-        def late_product(s, t):
-            product(prods[:, ROW * s + EARLY + LATE * t : ROW * s + EARLY + LATE * (t + 1)], s, t, EARLY, LATE)
+        def leave(piece, tiles, bank, copy, queue):
+            z_codes, z_scales, a, m = piece
+            acc = psum.tile([P, len(tiles), m], F32, name=f"acc{a}_{tiles[0]}", tag=f"bank{bank}")
+            res = keep.tile([P, len(tiles), m], F32, name=f"res{a}_{tiles[0]}")
+            seen.append(res)
+            for q, mt in enumerate(tiles):
+                nc.tensor.matmul_mx(
+                    out=acc[:, q, :],
+                    lhsT=w2_codes[:, P * mt : P * (mt + 1)].bitcast(FP8X4),
+                    lhsT_scale=w2_scales[:, P * mt : P * (mt + 1)],
+                    rhs=z_codes[:].bitcast(FP8X4),
+                    rhs_scale=z_scales[:],
+                    start=True,
+                    stop=True,
+                )
+            copy(res[:], acc[:])
+            queue.dma_start(out=out_rows[:, tiles[0] : tiles[-1] + 1, a : a + m], in_=res[:])
 
-        for s, t in ((0, 1), (1, 1), (1, 2), (1, 3)):
-            late_product(s, t)
-        finish([z.bitcast(BF16) for z in z_a], 0, (0, 1, 4, 5), [nc.scalar.copy] * 4, [nc.sync] * 4, "z_codes0")
-        late_product(0, 2)
-        late_product(0, 3)
-        finish([z_b[:].bitcast(BF16)], 256, (6,), [nc.scalar.copy], [nc.scalar], "k02")
+        first = quantise([z.bitcast(BF16) for z in z_a], 0, "z_codes0")
+        for mt, bank in enumerate((0, 1, 4, 5)):
+            leave(first, (mt,), bank, nc.scalar.copy, nc.sync)
+        late(1, 1)
+        late(1, 0)
+        late(0, 0)
+        middle = quantise([z_b[:].bitcast(BF16)], FIRST, "k10")
+        leave(middle, (0, 1, 2, 3), 6, nc.scalar.copy, nc.scalar)
         z_c = keep.tile([P, LATE, 4], BF16, name="z_c", align_bytes=64)
-        taps = [prods[:, ROW * s + EARLY : ROW * (s + 1)].rearrange("p (t c i) -> p c t i", t=4, i=4) for s in range(2)]
+        taps = [slot(s, 0, 4 * LATE).rearrange("p (t c i) -> p c t i", t=4, i=4) for s in range(2)]
         nc.vector.tensor_tensor(z_c[:].rearrange("p (c i) t -> p c t i", i=4), taps[0], taps[1], ADD)
-        finish(
-            [z_c[:].rearrange("p n t -> p (n t)")], EARLY, (7, 2, 3, 0),
-            [nc.vector.tensor_copy] * 4, [nc.sync] * 4, "z_codes2",
-        )
+        last = quantise([z_c[:].rearrange("p n t -> p (n t)")], EARLY, "z_codes2")
+        for mt, bank in enumerate((7, 2, 3, 0)):
+            leave(last, (mt,), bank, nc.vector.tensor_copy, nc.sync)

@@ -1,7 +1,6 @@
 from contextlib import ExitStack
 
 import concourse.mybir as mybir
-from concourse.masks import make_identity
 
 K, T, S, N, H, U = 512, 2048, 512, 512, 512, 512
 FLOPS = 2 * K * H * S + 2 * H * N * S
@@ -15,10 +14,9 @@ U8 = mybir.dt.uint8
 FP8X4 = mybir.dt.float8_e4m3fn_x4
 MULT = mybir.AluOpType.mult
 ADD = mybir.AluOpType.add
+COPY = mybir.ActivationFunctionType.Copy
 P = 128
-EARLY = 384
-LATE = S - EARLY
-FIRST = 256
+PIECE = 128
 
 
 def tile_picked_dynk8_none_p_kernel(
@@ -36,19 +34,16 @@ def tile_picked_dynk8_none_p_kernel(
         p2_t = lists.tile([P, S // 16], U16, name="p2_t")
 
         k_win = [[keep.tile([P, 2 * U], F32, name=f"k_win{s}_{t}") for t in range(4)] for s in range(2)]
-        k_rows = [kern.rearrange("(g t f) u -> t g f u", t=4, f=4) for kern in (kern1, kern2)]
+        k_rows = [kern.rearrange("(p t) u -> t p u", t=4) for kern in (kern1, kern2)]
         xs_win = keep.tile([P, T], U8, name="xs_win")
         xw_win = keep.tile([P, T], U32, name="xw_win")
         xw_rows = x_words[0].rearrange("p n t -> p (n t)").bitcast(I32)
-        w1_raw = keep.tile([P, 4, H], F32, name="w1_raw")
+        w1_raw = [keep.tile([P, 4, H // 2], F32, name=f"w1_raw{h}") for h in range(2)]
         w1_rows = w1.rearrange("(p j) c -> p j c", j=4)
-        w2_raw = keep.tile([P, 4, N], F32, name="w2_raw", tag="w2_raw")
-        w2_rows = w2.rearrange("(g t f) u -> t g f u", t=4, f=4)
+        w2_raw = keep.tile([P, 4, N], F32, name="w2_raw")
         xq_scales = keep.tile([P, S], U8, name="xq_scales", align_bytes=64)
-        ident = keep.tile([P, P], F32, name="ident")
         nc.gpsimd.memset(xs_win[:].bitcast(I32), 0)
         nc.gpsimd.memset(xq_scales[:].bitcast(I32), 0)
-        make_identity(nc, ident[:])
 
         def load_k(s, t):
             nc.sync.dma_start(out=k_win[s][t][:, 0:U], in_=k_rows[s][t])
@@ -56,63 +51,68 @@ def tile_picked_dynk8_none_p_kernel(
         load_k(0, 3)
         nc.sync.dma_start(cls_t[:], cls)
         nc.sync.dma_start(offs_t[:], offs)
-        load_k(0, 2)
         nc.sync.dma_start(out=xs_win[0:P:8, :].bitcast(I32), in_=x_scales[0].bitcast(I32))
-        load_k(0, 1)
-        load_k(0, 0)
-        nc.sync.dma_start(out=w1_raw[:], in_=w1_rows)
-        load_k(1, 3)
-        load_k(1, 2)
         nc.sync.dma_start(out=xw_win[:].bitcast(I32), in_=xw_rows)
-        load_k(1, 1)
-        load_k(1, 0)
+        load_k(1, 3)
+        for h in range(2):
+            nc.sync.dma_start(out=w1_raw[h][:], in_=w1_rows[:, :, h * H // 2 : (h + 1) * H // 2])
+        load_k(0, 2)
         nc.sync.dma_start(p1_t[:], p1)
         nc.sync.dma_start(p2_t[:], p2)
-        for t in range(4):
-            nc.sync.dma_start(out=w2_raw[:, t, :], in_=w2_rows[t])
+        load_k(1, 2)
+        for t in (1, 0):
+            load_k(0, t)
+            load_k(1, t)
+        nc.sync.dma_start(out=w2_raw[:], in_=w2.rearrange("(p j) c -> p j c", j=4))
 
         k_got = [[None] * 4, [None] * 4]
 
-        def gather_k(s, t):
-            k_got[s][t] = keep.tile([P, S], F32, name=f"k_got{s}_{t}", tag=f"k{s}{t}", align_bytes=64)
-            nc.vector.tensor_copy(k_got[s][t][:], k_win[s][t][:].indirect(cls_t[:]))
+        def gather_k(s, t, on_scalar=True, tag=None):
+            k_got[s][t] = keep.tile([P, S], F32, name=f"k_got{s}_{t}", tag=tag or f"k{s}{t}", align_bytes=64)
+            window = k_win[s][t][:].indirect(cls_t[:])
+            if on_scalar:
+                nc.scalar.activation(k_got[s][t][:], window, COPY)
+            else:
+                nc.vector.tensor_copy(k_got[s][t][:], window)
 
         gather_k(0, 3)
-        gather_k(0, 2)
         xs_got = keep.tile([P, S], U8, name="xs_got", align_bytes=64)
         nc.vector.tensor_copy(xs_got[:], xs_win[:].indirect(offs_t[:]))
         for r in range(4):
             nc.scalar.dma_start(out=xq_scales[r:P:32, :].bitcast(I32), in_=xs_got[8 * r : P : 32, :].bitcast(I32))
-        gather_k(0, 1)
-        gather_k(0, 0)
-        gather_k(1, 3)
-        gather_k(1, 2)
-
-        w1_codes, w1_scales = [None] * 2, [None] * 2
-        for u in (1, 0):
-            w1_bf = keep.tile([P, 2, P, 4], BF16, name=f"w1_bf{u}", align_bytes=64)
-            nc.scalar.copy(
-                out=w1_bf[:].rearrange("p t (g f) j -> p t g j f", f=4),
-                in_=w1_raw[:].rearrange("p j (g t f) -> p t g j f", t=4, f=4)[:, 2 * u : 2 * u + 2],
-            )
-            w1_codes[u] = keep.tile([P, 2 * P], U32, name=f"w1_codes{u}", align_bytes=64)
-            w1_scales[u] = keep.tile([P, 2 * P], U8, name=f"w1_scales{u}", align_bytes=64)
-            nc.vector.quantize_mx(
-                out=w1_codes[u][:].bitcast(FP8X4), scales=w1_scales[u][:], in_=w1_bf[:].rearrange("p t m j -> p (t m j)")
-            )
         xq_words = keep.tile([P, S], U32, name="xq_words", align_bytes=64)
         nc.vector.tensor_copy(xq_words[:], xw_win[:].indirect(offs_t[:]))
-        gather_k(1, 1)
-        gather_k(1, 0)
+        gather_k(1, 3)
 
-        y_win = [keep.tile([P, 2 * S if t == 3 else S], F32, name=f"y_win{t}") for t in range(4)]
-        for t in (3, 2, 1, 0):
-            u, e = divmod(t, 2)
-            bank = psum.tile([P, S], F32, name=f"ybank{t}", tag=f"bank{3 - t}")
+        w1_bf = keep.tile([P, 4, P, 4], BF16, name="w1_bf", align_bytes=64)
+        for h in range(2):
+            nc.vector.tensor_copy(
+                w1_bf[:, :, h * P // 2 : (h + 1) * P // 2, :].rearrange("p t m j -> p m j t"),
+                w1_raw[h][:].rearrange("p j (m t) -> p m j t", t=4),
+            )
+        w1_codes, w1_scales = [None] * 4, [None] * 4
+        for first, count in ((3, 1), (0, 3)):
+            codes = keep.tile([P, count * P], U32, name=f"w1_codes{first}", tag=f"w1_codes{first}", align_bytes=64)
+            scales = keep.tile([P, count * P], U8, name=f"w1_scales{first}", align_bytes=64)
+            nc.vector.quantize_mx(
+                out=codes[:].bitcast(FP8X4),
+                scales=scales[:],
+                in_=w1_bf[:, first : first + count].rearrange("p t m j -> p (t m j)"),
+            )
+            for e in range(count):
+                w1_codes[first + e] = codes[:, P * e : P * (e + 1)]
+                w1_scales[first + e] = scales[:, P * e : P * (e + 1)]
+        gather_k(0, 2)
+        gather_k(1, 2, on_scalar=False, tag="w1_raw_tail")
+
+        y_win = [keep.tile([P, 2 * S], F32, name=f"y_win{t}") for t in range(4)]
+
+        def project(t):
+            bank = psum.tile([P, S], F32, name=f"ybank{t}", tag=f"bank{t}")
             nc.tensor.matmul_mx(
                 out=bank[:],
-                lhsT=w1_codes[u][:, P * e : P * (e + 1)].bitcast(FP8X4),
-                lhsT_scale=w1_scales[u][:, P * e : P * (e + 1)],
+                lhsT=w1_codes[t].bitcast(FP8X4),
+                lhsT_scale=w1_scales[t],
                 rhs=xq_words[:].bitcast(FP8X4),
                 rhs_scale=xq_scales[:],
                 start=True,
@@ -120,121 +120,64 @@ def tile_picked_dynk8_none_p_kernel(
             )
             nc.scalar.copy(out=y_win[t][:, 0:S], in_=bank[:])
 
-        w2_bf = keep.tile([P, N, 4], BF16, name="w2_bf", align_bytes=64)
+        prods = [keep.tile([P, 4, S], F32, name=f"prods{s}", align_bytes=64) for s in range(2)]
+
+        def product(s, t):
+            nc.vector.tensor_tensor(prods[s][:, t, :], y_win[t][:].indirect((p1_t, p2_t)[s][:]), k_got[s][t][:], MULT)
+
+        project(3)
+        project(2)
+        gather_k(0, 1, tag="w1_codes3")
+        project(1)
+        gather_k(1, 1)
+        project(0)
+        gather_k(0, 0)
+        gather_k(1, 0)
+        for t in (3, 2, 1, 0):
+            product(0, t)
+            product(1, t)
+
+        w2_bf = keep.tile([P, N, 4], BF16, name="w2_bf", tag="woven", align_bytes=64)
         nc.scalar.copy(
             out=w2_bf[:].rearrange("p (c i) j -> p c j i", i=4),
             in_=w2_raw[:].rearrange("p j (c i) -> p c j i", i=4),
         )
-
-        ROW = P + S
-        prods = keep.tile([P, 2 * ROW], F32, name="prods", align_bytes=64)
-
-        def slot(s, t, n=LATE):
-            return prods[:, ROW * s + P * (t + 1) : ROW * s + P * (t + 1) + n]
-
-        def product(dst, s, t, a, n):
-            places = (p1_t, p2_t)[s][:, a // 16 : (a + n) // 16]
-            nc.vector.tensor_tensor(dst, y_win[t][:].indirect(places), k_got[s][t][:, a : a + n], MULT)
-
-        sums = {}
-        back = [psum.tile([P, 2, P], F32, name=f"back{jb}", tag=f"bank{(7, 2, 3)[jb]}")[:] for jb in range(3)]
-
-        def open_sums(u):
-            for jb in range(3):
-                sums[u, jb] = psum.tile([P, 2, P], F32, name=f"sums{u}_{jb}", tag=f"bank{4 + jb}")[:]
-
-        def turn(src, s, t, jb):
-            nc.tensor.matmul(sums[t // 2, jb][:, t % 2, :], src, ident[:], start=(s == 0), stop=(s == 1), is_transpose=True)
-
-        def turn_back(u, jb, pairs):
-            nc.scalar.copy(pairs.rearrange("j (p e) -> j p e", e=2), sums[u, jb].rearrange("j e p -> j p e"))
-            nc.tensor.transpose(back[jb][:, u, :], pairs.bitcast(F32), ident[:])
-
-        def weave(dst, jb):
-            nc.scalar.copy(dst.rearrange("p (n u) -> p n u", u=2), back[jb].rearrange("p u n -> p n u"))
-
-        def early(t, a, n, in_slots):
-            for s in range(2):
-                if in_slots:
-                    dst = slot(s, 0, n)
-                else:
-                    dst = keep.tile([P, n], F32, name=f"early{t}_{a}_{s}", align_bytes=64)[:]
-                product(dst, s, t, a, n)
-                for jb in range(a // P, min((a + n) // P, 3)):
-                    turn(dst[:, P * jb - a : P * (jb + 1) - a], s, t, jb)
-
-        open_sums(1)
-        early(3, 0, S, True)
-        early(2, 0, EARLY, False)
-        turned = keep.tile([P, 6 * P], BF16, name="turned1", tag="w2_raw")
-        for jb in range(3):
-            turn_back(1, jb, turned[:, 2 * P * jb : 2 * P * (jb + 1)])
-
-        open_sums(0)
-        early(1, 0, EARLY, False)
-        early(0, 0, FIRST, False)
-        early(0, FIRST, P, False)
-        turned = keep.tile([P, 6 * P], BF16, name="turned0", tag="w2_raw")
-        for jb in range(3):
-            turn_back(0, jb, turned[:, 2 * P * jb : 2 * P * (jb + 1)])
-        z_a = [slot(1, 0, 2 * P), slot(0, -1, 2 * P)]
-        for jb in range(2):
-            weave(z_a[jb], jb)
-        z_b = keep.tile([P, 2 * P], F32, name="z_b", align_bytes=64)
-        weave(z_b[:], 2)
-
-        def late(s, t):
-            product(slot(s, t), s, t, EARLY, LATE)
-
-        late(0, 2)
-        late(1, 2)
-        late(0, 1)
         w2_codes = keep.tile([P, N], U32, name="w2_codes", align_bytes=64)
         w2_scales = keep.tile([P, N], U8, name="w2_scales", align_bytes=64)
         nc.vector.quantize_mx(
             out=w2_codes[:].bitcast(FP8X4), scales=w2_scales[:], in_=w2_bf[:].rearrange("p n j -> p (n j)")
         )
         out_rows = out.rearrange("(mt p) j -> p mt j", p=P)
-        seen = []
+        pieces = S // PIECE
+        z_all = keep.tile([P, S, 4], BF16, name="z_all", tag="woven", align_bytes=64)
+        z_bf = [z_all[:, PIECE * b : PIECE * (b + 1), :] for b in range(pieces)]
 
-        def quantise(blocks, a, tag):
-            m = P * len(blocks)
-            z_codes = keep.tile([P, m], U32, name=f"z_codes{a}", tag=tag, align_bytes=64)
-            z_scales = keep.tile([P, m], U8, name=f"z_scales{a}", align_bytes=64)
-            for b, z_bf in enumerate(blocks):
-                cols = slice(P * b, P * (b + 1))
-                nc.vector.quantize_mx(out=z_codes[:, cols].bitcast(FP8X4), scales=z_scales[:, cols], in_=z_bf)
-            return z_codes, z_scales, a, m
+        def add(b):
+            taps = [prods[s][:, :, PIECE * b : PIECE * (b + 1)].rearrange("p t (c i) -> p c t i", i=4) for s in range(2)]
+            nc.vector.tensor_tensor(z_bf[b].rearrange("p (c i) t -> p c t i", i=4), taps[0], taps[1], ADD)
 
-        def leave(piece, tiles, bank, copy, queue):
-            z_codes, z_scales, a, m = piece
-            acc = psum.tile([P, len(tiles), m], F32, name=f"acc{a}_{tiles[0]}", tag=f"bank{bank}")
-            res = keep.tile([P, len(tiles), m], F32, name=f"res{a}_{tiles[0]}")
-            seen.append(res)
-            for q, mt in enumerate(tiles):
-                nc.tensor.matmul_mx(
-                    out=acc[:, q, :],
-                    lhsT=w2_codes[:, P * mt : P * (mt + 1)].bitcast(FP8X4),
-                    lhsT_scale=w2_scales[:, P * mt : P * (mt + 1)],
-                    rhs=z_codes[:].bitcast(FP8X4),
-                    rhs_scale=z_scales[:],
-                    start=True,
-                    stop=True,
-                )
-            copy(res[:], acc[:])
-            queue.dma_start(out=out_rows[:, tiles[0] : tiles[-1] + 1, a : a + m], in_=res[:])
+        def leave(b, parts):
+            z_codes = keep.tile([P, PIECE], U32, name=f"z_codes{b}", align_bytes=64)
+            z_scales = keep.tile([P, PIECE], U8, name=f"z_scales{b}", align_bytes=64)
+            nc.vector.quantize_mx(out=z_codes[:].bitcast(FP8X4), scales=z_scales[:], in_=z_bf[b].rearrange("p n t -> p (n t)"))
+            for tiles, bank, copy in parts:
+                acc = psum.tile([P, len(tiles), PIECE], F32, name=f"acc{b}_{tiles[0]}", tag=f"bank{bank}")
+                res = keep.tile([P, len(tiles), PIECE], F32, name=f"res{b}_{tiles[0]}")
+                for q, mt in enumerate(tiles):
+                    nc.tensor.matmul_mx(
+                        out=acc[:, q, :],
+                        lhsT=w2_codes[:, P * mt : P * (mt + 1)].bitcast(FP8X4),
+                        lhsT_scale=w2_scales[:, P * mt : P * (mt + 1)],
+                        rhs=z_codes[:].bitcast(FP8X4),
+                        rhs_scale=z_scales[:],
+                        start=True,
+                        stop=True,
+                    )
+                copy(res[:], acc[:])
+                nc.sync.dma_start(out=out_rows[:, tiles[0] : tiles[-1] + 1, PIECE * b : PIECE * (b + 1)], in_=res[:])
 
-        first = quantise([z.bitcast(BF16) for z in z_a], 0, "z_codes0")
-        for mt, bank in enumerate((0, 1, 4, 5)):
-            leave(first, (mt,), bank, nc.scalar.copy, nc.sync)
-        late(1, 1)
-        late(1, 0)
-        late(0, 0)
-        middle = quantise([z_b[:].bitcast(BF16)], FIRST, "k10")
-        leave(middle, (0, 1, 2, 3), 6, nc.scalar.copy, nc.scalar)
-        z_c = keep.tile([P, LATE, 4], BF16, name="z_c", align_bytes=64)
-        taps = [slot(s, 0, 4 * LATE).rearrange("p (t c i) -> p c t i", t=4, i=4) for s in range(2)]
-        nc.vector.tensor_tensor(z_c[:].rearrange("p (c i) t -> p c t i", i=4), taps[0], taps[1], ADD)
-        last = quantise([z_c[:].rearrange("p n t -> p (n t)")], EARLY, "z_codes2")
-        for mt, bank in enumerate((7, 2, 3, 0)):
-            leave(last, (mt,), bank, nc.vector.tensor_copy, nc.sync)
+        add(0)
+        for b in range(pieces - 1):
+            add(b + 1)
+            leave(b, [((0, 1, 2, 3), 4 + b, nc.scalar.copy)])
+        leave(pieces - 1, [((0, 1), 7, nc.vector.tensor_copy), ((2, 3), 0, nc.vector.tensor_copy)])

@@ -16,7 +16,7 @@ MULT = mybir.AluOpType.mult
 ADD = mybir.AluOpType.add
 COPY = mybir.ActivationFunctionType.Copy
 P = 128
-PIECE = 128
+HALF = 256
 
 
 def tile_picked_dynk8_none_p_kernel(
@@ -33,7 +33,7 @@ def tile_picked_dynk8_none_p_kernel(
         p1_t = lists.tile([P, S // 16], U16, name="p1_t")
         p2_t = lists.tile([P, S // 16], U16, name="p2_t")
 
-        k_win = [[keep.tile([P, 2 * U], F32, name=f"k_win{s}_{t}") for t in range(4)] for s in range(2)]
+        k_win = [[keep.tile([P, 2 * U], F32, name=f"k_win{s}_{t}", tag=f"k_win{s}_{t}") for t in range(4)] for s in range(2)]
         k_rows = [kern.rearrange("(p t) u -> t p u", t=4) for kern in (kern1, kern2)]
         xs_win = keep.tile([P, T], U8, name="xs_win")
         xw_win = keep.tile([P, T], U32, name="xw_win")
@@ -122,8 +122,11 @@ def tile_picked_dynk8_none_p_kernel(
 
         prods = [keep.tile([P, 4, S], F32, name=f"prods{s}", align_bytes=64) for s in range(2)]
 
-        def product(s, t):
-            nc.vector.tensor_tensor(prods[s][:, t, :], y_win[t][:].indirect((p1_t, p2_t)[s][:]), k_got[s][t][:], MULT)
+        def neighbours(s, t, a, n):
+            return y_win[t][:].indirect((p1_t, p2_t)[s][:, a // 16 : (a + n) // 16])
+
+        def product(s, t, a, n):
+            nc.vector.tensor_tensor(prods[s][:, t, a : a + n], neighbours(s, t, a, n), k_got[s][t][:, a : a + n], MULT)
 
         project(3)
         project(2)
@@ -133,9 +136,33 @@ def tile_picked_dynk8_none_p_kernel(
         project(0)
         gather_k(0, 0)
         gather_k(1, 0)
-        for t in (3, 2, 1, 0):
-            product(0, t)
-            product(1, t)
+        for t in (3, 2):
+            for s in range(2):
+                product(s, t, 0, S)
+        for t in (1, 0):
+            for s in range(2):
+                product(s, t, 0, HALF)
+        product(1, 0, HALF, HALF)
+
+        def add(z_bf, a, n):
+            taps = [prods[s][:, :, a : a + n].rearrange("p t (c i) -> p c t i", i=4) for s in range(2)]
+            nc.vector.tensor_tensor(z_bf.rearrange("p (c i) t -> p c t i", i=4), taps[0], taps[1], ADD)
+
+        def quantise(z_bf, a, n):
+            z_codes = keep.tile([P, n], U32, name=f"z_codes{a}", align_bytes=64)
+            z_scales = keep.tile([P, n], U8, name=f"z_scales{a}", align_bytes=64)
+            nc.vector.quantize_mx(out=z_codes[:].bitcast(FP8X4), scales=z_scales[:], in_=z_bf.rearrange("p n t -> p (n t)"))
+            return z_codes, z_scales, a, n
+
+        z_first = keep.tile([P, HALF, 4], BF16, name="z_first", align_bytes=64)
+        add(z_first[:], 0, HALF)
+
+        plain = ((0, 1), (1, 1), (0, 0))
+        y_got = keep.tile([P, len(plain), HALF], F32, name="y_got", tag="k_win1_0")
+        for q, (s, t) in enumerate(plain):
+            nc.scalar.activation(y_got[:, q, :], neighbours(s, t, HALF, HALF), COPY)
+            nc.vector.tensor_tensor(prods[s][:, t, HALF:S], y_got[:, q, :], k_got[s][t][:, HALF:S], MULT)
+        first = quantise(z_first[:], 0, HALF)
 
         w2_bf = keep.tile([P, N, 4], BF16, name="w2_bf", tag="woven", align_bytes=64)
         nc.scalar.copy(
@@ -148,36 +175,31 @@ def tile_picked_dynk8_none_p_kernel(
             out=w2_codes[:].bitcast(FP8X4), scales=w2_scales[:], in_=w2_bf[:].rearrange("p n j -> p (n j)")
         )
         out_rows = out.rearrange("(mt p) j -> p mt j", p=P)
-        pieces = S // PIECE
-        z_all = keep.tile([P, S, 4], BF16, name="z_all", tag="woven", align_bytes=64)
-        z_bf = [z_all[:, PIECE * b : PIECE * (b + 1), :] for b in range(pieces)]
 
-        def add(b):
-            taps = [prods[s][:, :, PIECE * b : PIECE * (b + 1)].rearrange("p t (c i) -> p c t i", i=4) for s in range(2)]
-            nc.vector.tensor_tensor(z_bf[b].rearrange("p (c i) t -> p c t i", i=4), taps[0], taps[1], ADD)
+        def leave(piece, tiles, bank, copy):
+            z_codes, z_scales, a, n = piece
+            acc = psum.tile([P, len(tiles), n], F32, name=f"acc{a}_{tiles[0]}", tag=f"bank{bank}")
+            res = keep.tile([P, len(tiles), n], F32, name=f"res{a}_{tiles[0]}")
+            for q, mt in enumerate(tiles):
+                nc.tensor.matmul_mx(
+                    out=acc[:, q, :],
+                    lhsT=w2_codes[:, P * mt : P * (mt + 1)].bitcast(FP8X4),
+                    lhsT_scale=w2_scales[:, P * mt : P * (mt + 1)],
+                    rhs=z_codes[:].bitcast(FP8X4),
+                    rhs_scale=z_scales[:],
+                    start=True,
+                    stop=True,
+                )
+            copy(res[:], acc[:])
+            nc.sync.dma_start(out=out_rows[:, tiles[0] : tiles[-1] + 1, a : a + n], in_=res[:])
 
-        def leave(b, parts):
-            z_codes = keep.tile([P, PIECE], U32, name=f"z_codes{b}", align_bytes=64)
-            z_scales = keep.tile([P, PIECE], U8, name=f"z_scales{b}", align_bytes=64)
-            nc.vector.quantize_mx(out=z_codes[:].bitcast(FP8X4), scales=z_scales[:], in_=z_bf[b].rearrange("p n t -> p (n t)"))
-            for tiles, bank, copy in parts:
-                acc = psum.tile([P, len(tiles), PIECE], F32, name=f"acc{b}_{tiles[0]}", tag=f"bank{bank}")
-                res = keep.tile([P, len(tiles), PIECE], F32, name=f"res{b}_{tiles[0]}")
-                for q, mt in enumerate(tiles):
-                    nc.tensor.matmul_mx(
-                        out=acc[:, q, :],
-                        lhsT=w2_codes[:, P * mt : P * (mt + 1)].bitcast(FP8X4),
-                        lhsT_scale=w2_scales[:, P * mt : P * (mt + 1)],
-                        rhs=z_codes[:].bitcast(FP8X4),
-                        rhs_scale=z_scales[:],
-                        start=True,
-                        stop=True,
-                    )
-                copy(res[:], acc[:])
-                nc.sync.dma_start(out=out_rows[:, tiles[0] : tiles[-1] + 1, PIECE * b : PIECE * (b + 1)], in_=res[:])
-
-        add(0)
-        for b in range(pieces - 1):
-            add(b + 1)
-            leave(b, [((0, 1, 2, 3), 4 + b, nc.scalar.copy)])
-        leave(pieces - 1, [((0, 1), 7, nc.vector.tensor_copy), ((2, 3), 0, nc.vector.tensor_copy)])
+        leave(first, (0, 1), 4, nc.scalar.copy)
+        leave(first, (2, 3), 5, nc.scalar.copy)
+        z_rest = keep.tile([P, HALF, 4], BF16, name="z_rest", tag="woven", align_bytes=64)
+        add(z_rest[:, 0:P, :], HALF, P)
+        middle = quantise(z_rest[:, 0:P, :], HALF, P)
+        leave(middle, (0, 1, 2, 3), 6, nc.scalar.copy)
+        add(z_rest[:, P:HALF, :], HALF + P, P)
+        last = quantise(z_rest[:, P:HALF, :], HALF + P, P)
+        leave(last, (0, 1), 7, nc.vector.tensor_copy)
+        leave(last, (2, 3), 0, nc.vector.tensor_copy)

@@ -34,7 +34,7 @@ def tile_picked_dynk8_none_p_kernel(
         p2_t = lists.tile([P, S // 16], U16, name="p2_t")
 
         k_win = [[keep.tile([P, 2 * U], F32, name=f"k_win{s}_{t}", tag=f"k_win{s}_{t}") for t in range(4)] for s in range(2)]
-        k_rows = [kern.rearrange("(p t) u -> t p u", t=4) for kern in (kern1, kern2)]
+        k_rows = [kern.rearrange("(g t f) u -> t g f u", t=4, f=4) for kern in (kern1, kern2)]
         xs_win = keep.tile([P, T], U8, name="xs_win")
         xw_win = keep.tile([P, T], U32, name="xw_win")
         xw_rows = x_words[0].rearrange("p n t -> p (n t)").bitcast(I32)
@@ -50,10 +50,10 @@ def tile_picked_dynk8_none_p_kernel(
 
         load_k(0, 3)
         nc.sync.dma_start(cls_t[:], cls)
+        load_k(1, 3)
         nc.sync.dma_start(offs_t[:], offs)
         nc.sync.dma_start(out=xs_win[0:P:8, :].bitcast(I32), in_=x_scales[0].bitcast(I32))
         nc.sync.dma_start(out=xw_win[:].bitcast(I32), in_=xw_rows)
-        load_k(1, 3)
         for h in range(2):
             nc.sync.dma_start(out=w1_raw[h][:], in_=w1_rows[:, :, h * H // 2 : (h + 1) * H // 2])
         load_k(0, 2)
@@ -63,7 +63,9 @@ def tile_picked_dynk8_none_p_kernel(
         for t in (1, 0):
             load_k(0, t)
             load_k(1, t)
-        nc.sync.dma_start(out=w2_raw[:], in_=w2.rearrange("(p j) c -> p j c", j=4))
+        w2_rows = w2.rearrange("(g t f) u -> t g f u", t=4, f=4)
+        for t in range(4):
+            nc.sync.dma_start(out=w2_raw[:, t, :], in_=w2_rows[t])
 
         k_got = [[None] * 4, [None] * 4]
 
@@ -80,16 +82,21 @@ def tile_picked_dynk8_none_p_kernel(
         nc.vector.tensor_copy(xs_got[:], xs_win[:].indirect(offs_t[:]))
         for r in range(4):
             nc.scalar.dma_start(out=xq_scales[r:P:32, :].bitcast(I32), in_=xs_got[8 * r : P : 32, :].bitcast(I32))
+        gather_k(1, 3)
         xq_words = keep.tile([P, S], U32, name="xq_words", align_bytes=64)
         nc.vector.tensor_copy(xq_words[:], xw_win[:].indirect(offs_t[:]))
-        gather_k(1, 3)
 
         w1_bf = keep.tile([P, 4, P, 4], BF16, name="w1_bf", align_bytes=64)
-        for h in range(2):
-            nc.vector.tensor_copy(
-                w1_bf[:, :, h * P // 2 : (h + 1) * P // 2, :].rearrange("p t m j -> p m j t"),
-                w1_raw[h][:].rearrange("p j (m t) -> p m j t", t=4),
+
+        def cast_w1(copy, h, g0, g1):
+            copy(
+                w1_bf[:, :, 64 * h + 4 * g0 : 64 * h + 4 * g1, :].rearrange("p t (g f) j -> p g t j f", f=4),
+                w1_raw[h][:, :, 16 * g0 : 16 * g1].rearrange("p j (g t f) -> p g t j f", t=4, f=4),
             )
+
+        cast_w1(nc.vector.tensor_copy, 0, 0, 16)
+        cast_w1(nc.vector.tensor_copy, 1, 0, 10)
+        cast_w1(nc.scalar.copy, 1, 10, 16)
         w1_codes, w1_scales = [None] * 4, [None] * 4
         for first, count in ((3, 1), (0, 3)):
             codes = keep.tile([P, count * P], U32, name=f"w1_codes{first}", tag=f"w1_codes{first}", align_bytes=64)

@@ -40,7 +40,7 @@ def tile_picked_dynk8_none_p_kernel(
         xw_rows = x_words[0].rearrange("p n t -> p (n t)").bitcast(I32)
         w1_raw = [keep.tile([P, 4, H // 2], F32, name=f"w1_raw{h}") for h in range(2)]
         w1_rows = w1.rearrange("(p j) c -> p j c", j=4)
-        w2_raw = keep.tile([P, 4, N], F32, name="w2_raw")
+        w2_raw = keep.tile([P, 4, N], F32, name="w2_raw", tag="w2_raw")
         xq_scales = keep.tile([P, S], U8, name="xq_scales", align_bytes=64)
         nc.gpsimd.memset(xs_win[:].bitcast(I32), 0)
         nc.gpsimd.memset(xq_scales[:].bitcast(I32), 0)
@@ -112,7 +112,7 @@ def tile_picked_dynk8_none_p_kernel(
         gather_k(0, 2)
         gather_k(1, 2, on_scalar=False, tag="w1_raw_tail")
 
-        y_win = [keep.tile([P, 2 * S], F32, name=f"y_win{t}") for t in range(4)]
+        y_win = [keep.tile([P, 2 * S if t >= 2 else S], F32, name=f"y_win{t}") for t in range(4)]
 
         def project(t):
             bank = psum.tile([P, S], F32, name=f"ybank{t}", tag=f"bank{t}")
@@ -164,13 +164,6 @@ def tile_picked_dynk8_none_p_kernel(
         z_first = keep.tile([P, HALF, 4], BF16, name="z_first", align_bytes=64)
         add(z_first[:], 0, HALF)
 
-        plain = ((0, 1), (1, 1), (0, 0))
-        y_got = keep.tile([P, len(plain), HALF], F32, name="y_got", tag="k_win1_0")
-        for q, (s, t) in enumerate(plain):
-            nc.scalar.activation(y_got[:, q, :], neighbours(s, t, HALF, HALF), COPY)
-            nc.vector.tensor_tensor(prods[s][:, t, HALF:S], y_got[:, q, :], k_got[s][t][:, HALF:S], MULT)
-        first = quantise(z_first[:], 0, HALF)
-
         w2_bf = keep.tile([P, N, 4], BF16, name="w2_bf", tag="woven", align_bytes=64)
         nc.scalar.copy(
             out=w2_bf[:].rearrange("p (c i) j -> p c j i", i=4),
@@ -181,32 +174,54 @@ def tile_picked_dynk8_none_p_kernel(
         nc.vector.quantize_mx(
             out=w2_codes[:].bitcast(FP8X4), scales=w2_scales[:], in_=w2_bf[:].rearrange("p n j -> p (n j)")
         )
+        first = quantise(z_first[:], 0, HALF)
+        plain = ((0, 1), (1, 1), (0, 0))
+        y_got = keep.tile([P, 2, len(plain), P], F32, name="y_got", tag="w2_raw")
+        for b in range(2):
+            for q, (s, t) in enumerate(plain):
+                nc.scalar.activation(y_got[:, b, q, :], neighbours(s, t, HALF + P * b, P), COPY)
+
+        def multiply(q, b):
+            s, t = plain[q]
+            places = slice(HALF + P * b, HALF + P * (b + 1))
+            nc.vector.tensor_tensor(prods[s][:, t, places], y_got[:, b, q, :], k_got[s][t][:, places], MULT)
+
         out_rows = out.rearrange("(mt p) j -> p mt j", p=P)
 
-        def leave(piece, tiles, bank, copy):
+        seen = []
+
+        def leave(piece, parts):
             z_codes, z_scales, a, n = piece
-            acc = psum.tile([P, len(tiles), n], F32, name=f"acc{a}_{tiles[0]}", tag=f"bank{bank}")
+            tiles = [mt for part, bank, copy in parts for mt in part]
             res = keep.tile([P, len(tiles), n], F32, name=f"res{a}_{tiles[0]}")
-            for q, mt in enumerate(tiles):
-                nc.tensor.matmul_mx(
-                    out=acc[:, q, :],
-                    lhsT=w2_codes[:, P * mt : P * (mt + 1)].bitcast(FP8X4),
-                    lhsT_scale=w2_scales[:, P * mt : P * (mt + 1)],
-                    rhs=z_codes[:].bitcast(FP8X4),
-                    rhs_scale=z_scales[:],
-                    start=True,
-                    stop=True,
-                )
-            copy(res[:], acc[:])
+            seen.append(res)
+            for part, bank, copy in parts:
+                acc = psum.tile([P, len(part), n], F32, name=f"acc{a}_{part[0]}", tag=f"bank{bank}")
+                for q, mt in enumerate(part):
+                    nc.tensor.matmul_mx(
+                        out=acc[:, q, :],
+                        lhsT=w2_codes[:, P * mt : P * (mt + 1)].bitcast(FP8X4),
+                        lhsT_scale=w2_scales[:, P * mt : P * (mt + 1)],
+                        rhs=z_codes[:].bitcast(FP8X4),
+                        rhs_scale=z_scales[:],
+                        start=True,
+                        stop=True,
+                    )
+                copy(res[:, part[0] - tiles[0] : part[-1] - tiles[0] + 1, :], acc[:])
             nc.sync.dma_start(out=out_rows[:, tiles[0] : tiles[-1] + 1, a : a + n], in_=res[:])
 
-        leave(first, (0, 1), 4, nc.scalar.copy)
-        leave(first, (2, 3), 5, nc.scalar.copy)
+        leave(first, [((0, 1), 4, nc.scalar.copy)])
+        leave(first, [((2, 3), 5, nc.scalar.copy)])
         z_rest = keep.tile([P, HALF, 4], BF16, name="z_rest", tag="woven", align_bytes=64)
+        for q in range(3):
+            multiply(q, 0)
+        multiply(0, 1)
         add(z_rest[:, 0:P, :], HALF, P)
+        multiply(1, 1)
+        multiply(2, 1)
         middle = quantise(z_rest[:, 0:P, :], HALF, P)
-        leave(middle, (0, 1, 2, 3), 6, nc.scalar.copy)
+        leave(middle, [((0, 1, 2, 3), 6, nc.scalar.copy)])
         add(z_rest[:, P:HALF, :], HALF + P, P)
         last = quantise(z_rest[:, P:HALF, :], HALF + P, P)
-        leave(last, (0, 1), 7, nc.vector.tensor_copy)
-        leave(last, (2, 3), 0, nc.vector.tensor_copy)
+        for mt, bank in enumerate((7, 0, 1, 2)):
+            leave(last, [((mt,), bank, (nc.vector.tensor_copy, nc.scalar.copy)[mt % 2])])

@@ -49,16 +49,16 @@ def tile_picked_dynk8_none_p_kernel(
             nc.sync.dma_start(out=k_win[s][t][:, 0:U], in_=k_rows[s][t])
 
         load_k(0, 3)
-        nc.sync.dma_start(cls_t[:], cls)
-        load_k(1, 3)
         nc.sync.dma_start(offs_t[:], offs)
+        nc.sync.dma_start(p1_t[:], p1)
         nc.sync.dma_start(out=xs_win[0:P:8, :].bitcast(I32), in_=x_scales[0].bitcast(I32))
+        nc.sync.dma_start(cls_t[:], cls)
+        nc.sync.dma_start(p2_t[:], p2)
+        load_k(1, 3)
         nc.sync.dma_start(out=xw_win[:].bitcast(I32), in_=xw_rows)
         for h in range(2):
             nc.sync.dma_start(out=w1_raw[h][:], in_=w1_rows[:, :, h * H // 2 : (h + 1) * H // 2])
         load_k(0, 2)
-        nc.sync.dma_start(p1_t[:], p1)
-        nc.sync.dma_start(p2_t[:], p2)
         load_k(1, 2)
         for t in (1, 0):
             load_k(0, t)
@@ -77,11 +77,11 @@ def tile_picked_dynk8_none_p_kernel(
             else:
                 nc.vector.tensor_copy(k_got[s][t][:], window)
 
-        gather_k(0, 3)
         xs_got = keep.tile([P, S], U8, name="xs_got", align_bytes=64)
         nc.vector.tensor_copy(xs_got[:], xs_win[:].indirect(offs_t[:]))
         for r in range(4):
             nc.scalar.dma_start(out=xq_scales[r:P:32, :].bitcast(I32), in_=xs_got[8 * r : P : 32, :].bitcast(I32))
+        gather_k(0, 3, on_scalar=False)
         gather_k(1, 3)
         xq_words = keep.tile([P, S], U32, name="xq_words", align_bytes=64)
         nc.vector.tensor_copy(xq_words[:], xw_win[:].indirect(offs_t[:]))

@@ -16,7 +16,8 @@ MULT = mybir.AluOpType.mult
 ADD = mybir.AluOpType.add
 COPY = mybir.ActivationFunctionType.Copy
 P = 128
-HALF = 256
+HALF = S // 2
+QUARTER = S // 4
 
 
 def tile_picked_dynk8_none_p_kernel(
@@ -26,6 +27,7 @@ def tile_picked_dynk8_none_p_kernel(
     with ExitStack() as ctx:
         lists = ctx.enter_context(tc.tile_pool(name="lists", bufs=1))
         keep = ctx.enter_context(tc.tile_pool(name="keep", bufs=1))
+        shared = ctx.enter_context(tc.tile_pool(name="shared", bufs=1))
         psum = ctx.enter_context(tc.psum_pool(name="psum", bufs=1))
 
         offs_t = lists.tile([P, S // 16], U16, name="offs_t")
@@ -33,14 +35,14 @@ def tile_picked_dynk8_none_p_kernel(
         p1_t = lists.tile([P, S // 16], U16, name="p1_t")
         p2_t = lists.tile([P, S // 16], U16, name="p2_t")
 
-        k_win = [[keep.tile([P, 2 * U], F32, name=f"k_win{s}_{t}", tag=f"k_win{s}_{t}") for t in range(4)] for s in range(2)]
+        k_win = [[keep.tile([P, 2 * U], F32, name=f"k_win{s}_{t}") for t in range(4)] for s in range(2)]
         k_rows = [kern.rearrange("(g t f) u -> t g f u", t=4, f=4) for kern in (kern1, kern2)]
         xs_win = keep.tile([P, T], U8, name="xs_win")
         xw_win = keep.tile([P, T], U32, name="xw_win")
-        xw_rows = x_words[0].rearrange("p n t -> p (n t)").bitcast(I32)
         w1_raw = [keep.tile([P, 4, H // 2], F32, name=f"w1_raw{h}") for h in range(2)]
         w1_rows = w1.rearrange("(p j) c -> p j c", j=4)
-        w2_raw = keep.tile([P, 4, N], F32, name="w2_raw", tag="w2_raw")
+        w2_raw = shared.tile([P, 4 * N], F32, name="w2_raw", offset=0, align_bytes=64)
+        w2_rows = w2.rearrange("(g t f) u -> t g f u", t=4, f=4)
         xq_scales = keep.tile([P, S], U8, name="xq_scales", align_bytes=64)
         nc.gpsimd.memset(xs_win[:].bitcast(I32), 0)
         nc.gpsimd.memset(xq_scales[:].bitcast(I32), 0)
@@ -48,41 +50,38 @@ def tile_picked_dynk8_none_p_kernel(
         def load_k(s, t):
             nc.sync.dma_start(out=k_win[s][t][:, 0:U], in_=k_rows[s][t])
 
-        load_k(0, 3)
+        load_k(0, 0)
         nc.sync.dma_start(offs_t[:], offs)
         nc.sync.dma_start(p1_t[:], p1)
         nc.sync.dma_start(out=xs_win[0:P:8, :].bitcast(I32), in_=x_scales[0].bitcast(I32))
         nc.sync.dma_start(cls_t[:], cls)
         nc.sync.dma_start(p2_t[:], p2)
-        load_k(1, 3)
-        nc.sync.dma_start(out=xw_win[:].bitcast(I32), in_=xw_rows)
+        load_k(1, 0)
+        nc.sync.dma_start(out=xw_win[:].bitcast(I32), in_=x_words[0].rearrange("p n t -> p (n t)").bitcast(I32))
         for h in range(2):
             nc.sync.dma_start(out=w1_raw[h][:], in_=w1_rows[:, :, h * H // 2 : (h + 1) * H // 2])
-        load_k(0, 2)
-        load_k(1, 2)
-        for t in (1, 0):
+        for t in range(1, 4):
             load_k(0, t)
             load_k(1, t)
-        w2_rows = w2.rearrange("(g t f) u -> t g f u", t=4, f=4)
         for t in range(4):
-            nc.sync.dma_start(out=w2_raw[:, t, :], in_=w2_rows[t])
+            nc.sync.dma_start(out=w2_raw[:, N * t : N * (t + 1)], in_=w2_rows[t])
 
         k_got = [[None] * 4, [None] * 4]
 
-        def gather_k(s, t, on_scalar=True, tag=None):
-            k_got[s][t] = keep.tile([P, S], F32, name=f"k_got{s}_{t}", tag=tag or f"k{s}{t}", align_bytes=64)
+        def gather_k(s, t, on_vector=False, tag=None):
+            k_got[s][t] = keep.tile([P, S], F32, name=f"k_got{s}_{t}", tag=tag or f"k_got{s}_{t}", align_bytes=64)
             window = k_win[s][t][:].indirect(cls_t[:])
-            if on_scalar:
-                nc.scalar.activation(k_got[s][t][:], window, COPY)
-            else:
+            if on_vector:
                 nc.vector.tensor_copy(k_got[s][t][:], window)
+            else:
+                nc.scalar.activation(k_got[s][t][:], window, COPY)
 
         xs_got = keep.tile([P, S], U8, name="xs_got", align_bytes=64)
         nc.vector.tensor_copy(xs_got[:], xs_win[:].indirect(offs_t[:]))
         for r in range(4):
             nc.scalar.dma_start(out=xq_scales[r:P:32, :].bitcast(I32), in_=xs_got[8 * r : P : 32, :].bitcast(I32))
-        gather_k(0, 3, on_scalar=False)
-        gather_k(1, 3)
+        gather_k(0, 0, on_vector=True)
+        gather_k(1, 0)
         xq_words = keep.tile([P, S], U32, name="xq_words", align_bytes=64)
         nc.vector.tensor_copy(xq_words[:], xw_win[:].indirect(offs_t[:]))
 
@@ -97,8 +96,8 @@ def tile_picked_dynk8_none_p_kernel(
         cast_w1(nc.vector.tensor_copy, 0, 0, 16)
         cast_w1(nc.vector.tensor_copy, 1, 0, 10)
         cast_w1(nc.scalar.copy, 1, 10, 16)
-        w1_codes, w1_scales = [None] * 4, [None] * 4
-        for first, count in ((3, 1), (0, 3)):
+        w1_codes, w1_scales = [], []
+        for first, count in ((0, 1), (1, 3)):
             codes = keep.tile([P, count * P], U32, name=f"w1_codes{first}", tag=f"w1_codes{first}", align_bytes=64)
             scales = keep.tile([P, count * P], U8, name=f"w1_scales{first}", align_bytes=64)
             nc.vector.quantize_mx(
@@ -106,16 +105,15 @@ def tile_picked_dynk8_none_p_kernel(
                 scales=scales[:],
                 in_=w1_bf[:, first : first + count].rearrange("p t m j -> p (t m j)"),
             )
-            for e in range(count):
-                w1_codes[first + e] = codes[:, P * e : P * (e + 1)]
-                w1_scales[first + e] = scales[:, P * e : P * (e + 1)]
-        gather_k(0, 2)
-        gather_k(1, 2, on_scalar=False, tag="w1_raw_tail")
+            w1_codes.extend(codes[:, P * e : P * (e + 1)] for e in range(count))
+            w1_scales.extend(scales[:, P * e : P * (e + 1)] for e in range(count))
+        gather_k(0, 1)
+        gather_k(1, 1, on_vector=True)
 
-        y_win = [keep.tile([P, 2 * S if t >= 2 else S], F32, name=f"y_win{t}") for t in range(4)]
+        y_win = [keep.tile([P, 2 * S if t < 2 else S], F32, name=f"y_win{t}", tag=f"y_win{t}") for t in range(4)]
 
         def project(t):
-            bank = psum.tile([P, S], F32, name=f"ybank{t}", tag=f"bank{t}")
+            bank = psum.tile([P, S], F32, name=f"y_bank{t}", tag=f"bank{t}")
             nc.tensor.matmul_mx(
                 out=bank[:],
                 lhsT=w1_codes[t].bitcast(FP8X4),
@@ -127,7 +125,19 @@ def tile_picked_dynk8_none_p_kernel(
             )
             nc.scalar.copy(out=y_win[t][:, 0:S], in_=bank[:])
 
-        prods = [keep.tile([P, 4, S], F32, name=f"prods{s}", align_bytes=64) for s in range(2)]
+        project(0)
+        project(1)
+        gather_k(0, 2, tag="w1_codes0")
+        project(2)
+        gather_k(1, 2)
+        project(3)
+        gather_k(0, 3)
+        gather_k(1, 3)
+
+        taps = keep.tile([P, 8 * S - QUARTER + 2 * N], F32, name="taps", align_bytes=64)
+        prods = [taps[:, 4 * S * (1 - s) : 4 * S * (2 - s)].rearrange("p (t n) -> p t n", t=4) for s in range(2)]
+        w2_bf = taps[:, 8 * S - QUARTER : 8 * S - QUARTER + 2 * N].bitcast(BF16).rearrange("p (n j) -> p n j", j=4)
+        z_rest = taps[:, 8 * S : 8 * S + 2 * HALF].bitcast(BF16).rearrange("p (n t) -> p n t", t=4)
 
         def neighbours(s, t, a, n):
             return y_win[t][:].indirect((p1_t, p2_t)[s][:, a // 16 : (a + n) // 16])
@@ -135,65 +145,60 @@ def tile_picked_dynk8_none_p_kernel(
         def product(s, t, a, n):
             nc.vector.tensor_tensor(prods[s][:, t, a : a + n], neighbours(s, t, a, n), k_got[s][t][:, a : a + n], MULT)
 
-        project(3)
-        project(2)
-        gather_k(0, 1, tag="w1_codes3")
-        project(1)
-        gather_k(1, 1)
-        project(0)
-        gather_k(0, 0)
-        gather_k(1, 0)
-        for t in (3, 2):
-            for s in range(2):
-                product(s, t, 0, S)
-        for t in (1, 0):
-            for s in range(2):
-                product(s, t, 0, HALF)
-        product(1, 0, HALF, HALF)
-
         def add(z_bf, a, n):
-            taps = [prods[s][:, :, a : a + n].rearrange("p t (c i) -> p c t i", i=4) for s in range(2)]
-            nc.vector.tensor_tensor(z_bf.rearrange("p (c i) t -> p c t i", i=4), taps[0], taps[1], ADD)
+            both = [prods[s][:, :, a : a + n].rearrange("p t (c i) -> p c t i", i=4) for s in range(2)]
+            nc.vector.tensor_tensor(z_bf.rearrange("p (c i) t -> p c t i", i=4), both[0], both[1], ADD)
 
-        def quantise(z_bf, a, n):
-            z_codes = keep.tile([P, n], U32, name=f"z_codes{a}", align_bytes=64)
+        def quantise(z_bf, a, n, z_codes):
             z_scales = keep.tile([P, n], U8, name=f"z_scales{a}", align_bytes=64)
-            nc.vector.quantize_mx(out=z_codes[:].bitcast(FP8X4), scales=z_scales[:], in_=z_bf.rearrange("p n t -> p (n t)"))
+            nc.vector.quantize_mx(out=z_codes.bitcast(FP8X4), scales=z_scales[:], in_=z_bf.rearrange("p n t -> p (n t)"))
             return z_codes, z_scales, a, n
 
+        for t in range(2):
+            for s in range(2):
+                product(s, t, 0, S)
+        for t in range(2, 4):
+            for s in range(2):
+                product(s, t, 0, HALF)
+        product(1, 3, HALF, HALF)
         z_first = keep.tile([P, HALF, 4], BF16, name="z_first", align_bytes=64)
         add(z_first[:], 0, HALF)
 
-        w2_bf = keep.tile([P, N, 4], BF16, name="w2_bf", tag="woven", align_bytes=64)
         nc.scalar.copy(
-            out=w2_bf[:].rearrange("p (c i) j -> p c j i", i=4),
-            in_=w2_raw[:].rearrange("p j (c i) -> p c j i", i=4),
+            out=w2_bf.rearrange("p (c i) j -> p c j i", i=4),
+            in_=w2_raw[:].rearrange("p (j c i) -> p c j i", j=4, i=4),
         )
         w2_codes = keep.tile([P, N], U32, name="w2_codes", align_bytes=64)
         w2_scales = keep.tile([P, N], U8, name="w2_scales", align_bytes=64)
-        nc.vector.quantize_mx(
-            out=w2_codes[:].bitcast(FP8X4), scales=w2_scales[:], in_=w2_bf[:].rearrange("p n j -> p (n j)")
-        )
-        first = quantise(z_first[:], 0, HALF)
-        plain = ((0, 1), (1, 1), (0, 0))
-        y_got = keep.tile([P, 2, len(plain), P], F32, name="y_got", tag="w2_raw")
+
+        def quantise_w2(a, b):
+            nc.vector.quantize_mx(
+                out=w2_codes[:, a:b].bitcast(FP8X4), scales=w2_scales[:, a:b], in_=w2_bf[:, a:b, :].rearrange("p n j -> p (n j)")
+            )
+
+        first_codes = shared.tile([P, HALF], U32, name="first_codes", offset=4096, align_bytes=64)
+        quantise_w2(0, N // 2)
+        first = quantise(z_first[:], 0, HALF, first_codes[:])
+        quantise_w2(N // 2, N)
+
+        plain = ((0, 2), (1, 2), (0, 3))
+        y_got = shared.tile([P, 2, 3, QUARTER], F32, name="y_got", offset=0, align_bytes=64)
         for b in range(2):
-            for q, (s, t) in enumerate(plain):
-                nc.scalar.activation(y_got[:, b, q, :], neighbours(s, t, HALF + P * b, P), COPY)
+            for q, (s, t) in enumerate(plain[: 3 - b]):
+                nc.scalar.activation(y_got[:, b, q, :], neighbours(s, t, HALF + QUARTER * b, QUARTER), COPY)
 
         def multiply(q, b):
             s, t = plain[q]
-            places = slice(HALF + P * b, HALF + P * (b + 1))
+            places = slice(HALF + QUARTER * b, HALF + QUARTER * (b + 1))
             nc.vector.tensor_tensor(prods[s][:, t, places], y_got[:, b, q, :], k_got[s][t][:, places], MULT)
 
         out_rows = out.rearrange("(mt p) j -> p mt j", p=P)
-
         seen = []
 
-        def leave(piece, parts):
+        def leave(piece, parts, tag=None):
             z_codes, z_scales, a, n = piece
             tiles = [mt for part, bank, copy in parts for mt in part]
-            res = keep.tile([P, len(tiles), n], F32, name=f"res{a}_{tiles[0]}")
+            res = keep.tile([P, len(tiles), n], F32, name=f"res{a}_{tiles[0]}", tag=tag or f"res{a}_{tiles[0]}")
             seen.append(res)
             for part, bank, copy in parts:
                 acc = psum.tile([P, len(part), n], F32, name=f"acc{a}_{part[0]}", tag=f"bank{bank}")
@@ -202,7 +207,7 @@ def tile_picked_dynk8_none_p_kernel(
                         out=acc[:, q, :],
                         lhsT=w2_codes[:, P * mt : P * (mt + 1)].bitcast(FP8X4),
                         lhsT_scale=w2_scales[:, P * mt : P * (mt + 1)],
-                        rhs=z_codes[:].bitcast(FP8X4),
+                        rhs=z_codes.bitcast(FP8X4),
                         rhs_scale=z_scales[:],
                         start=True,
                         stop=True,
@@ -210,18 +215,19 @@ def tile_picked_dynk8_none_p_kernel(
                 copy(res[:, part[0] - tiles[0] : part[-1] - tiles[0] + 1, :], acc[:])
             nc.sync.dma_start(out=out_rows[:, tiles[0] : tiles[-1] + 1, a : a + n], in_=res[:])
 
-        leave(first, [((0, 1), 4, nc.scalar.copy)])
+        leave(first, [((0, 1), 4, nc.scalar.copy)], tag="y_win2")
         leave(first, [((2, 3), 5, nc.scalar.copy)])
-        z_rest = keep.tile([P, HALF, 4], BF16, name="z_rest", tag="woven", align_bytes=64)
+        rest_codes = [keep.tile([P, QUARTER], U32, name=f"z_codes{b}", align_bytes=64) for b in range(2)]
         for q in range(3):
             multiply(q, 0)
         multiply(0, 1)
-        add(z_rest[:, 0:P, :], HALF, P)
+        add(z_rest[:, 0:QUARTER, :], HALF, QUARTER)
         multiply(1, 1)
-        multiply(2, 1)
-        middle = quantise(z_rest[:, 0:P, :], HALF, P)
-        leave(middle, [((0, 1, 2, 3), 6, nc.scalar.copy)])
-        add(z_rest[:, P:HALF, :], HALF + P, P)
-        last = quantise(z_rest[:, P:HALF, :], HALF + P, P)
-        for mt, bank in enumerate((7, 0, 1, 2)):
-            leave(last, [((mt,), bank, (nc.vector.tensor_copy, nc.scalar.copy)[mt % 2])])
+        product(0, 3, HALF + QUARTER, QUARTER)
+        middle = quantise(z_rest[:, 0:QUARTER, :], HALF, QUARTER, rest_codes[0][:])
+        leave(middle, [((0, 1), 6, nc.scalar.copy)])
+        leave(middle, [((2, 3), 3, nc.scalar.copy)])
+        add(z_rest[:, QUARTER:HALF, :], HALF + QUARTER, QUARTER)
+        last = quantise(z_rest[:, QUARTER:HALF, :], HALF + QUARTER, QUARTER, rest_codes[1][:])
+        leave(last, [((0,), 7, nc.vector.tensor_copy), ((1,), 0, nc.scalar.copy)])
+        leave(last, [((2,), 1, nc.vector.tensor_copy), ((3,), 2, nc.scalar.copy)])

from contextlib import ExitStack

import concourse.mybir as mybir

K, T, S, N, H, U = 512, 2048, 512, 512, 512, 512
FLOPS = 2 * K * H * S + 2 * H * N * S

F32 = mybir.dt.float32
BF16 = mybir.dt.bfloat16
I32 = mybir.dt.int32
U32 = mybir.dt.uint32
U16 = mybir.dt.uint16
U8 = mybir.dt.uint8
FP8X4 = mybir.dt.float8_e4m3fn_x4
MULT = mybir.AluOpType.mult
ADD = mybir.AluOpType.add
COPY = mybir.ActivationFunctionType.Copy
P = 128
HALF = S // 2
QUARTER = S // 4


def tile_picked_dynk8_none_p_kernel(
    tc, x_words, x_scales, w1, kern1, kern2, w2, offs, cls, p1, p2, out
):
    nc = tc.nc
    with ExitStack() as ctx:
        lists = ctx.enter_context(tc.tile_pool(name="lists", bufs=1))
        keep = ctx.enter_context(tc.tile_pool(name="keep", bufs=1))
        shared = ctx.enter_context(tc.tile_pool(name="shared", bufs=1))
        psum = ctx.enter_context(tc.psum_pool(name="psum", bufs=1))

        offs_t = lists.tile([P, S // 16], U16, name="offs_t")
        cls_t = lists.tile([P, S // 16], U16, name="cls_t")
        p1_t = lists.tile([P, S // 16], U16, name="p1_t")
        p2_t = lists.tile([P, S // 16], U16, name="p2_t")

        k_win = [[keep.tile([P, 2 * U], F32, name=f"k_win{s}_{t}") for t in range(4)] for s in range(2)]
        k_rows = [kern.rearrange("(g t f) u -> t g f u", t=4, f=4) for kern in (kern1, kern2)]
        xs_win = keep.tile([P, T], U8, name="xs_win")
        xw_win = keep.tile([P, T], U32, name="xw_win")
        w1_raw = [keep.tile([P, 4, H // 2], F32, name=f"w1_raw{h}") for h in range(2)]
        w1_rows = w1.rearrange("(p j) c -> p j c", j=4)
        w2_raw = shared.tile([P, 4 * N], F32, name="w2_raw", offset=0, align_bytes=64)
        w2_rows = w2.rearrange("(g t f) u -> t g f u", t=4, f=4)
        xq_scales = keep.tile([P, S], U8, name="xq_scales", align_bytes=64)
        nc.gpsimd.memset(xs_win[:].bitcast(I32), 0)
        nc.gpsimd.memset(xq_scales[:].bitcast(I32), 0)

        def load_k(s, t):
            nc.sync.dma_start(out=k_win[s][t][:, 0:U], in_=k_rows[s][t])

        load_k(0, 0)
        nc.sync.dma_start(offs_t[:], offs)
        nc.sync.dma_start(p1_t[:], p1)
        nc.sync.dma_start(out=xs_win[0:P:8, :].bitcast(I32), in_=x_scales[0].bitcast(I32))
        nc.sync.dma_start(cls_t[:], cls)
        nc.sync.dma_start(p2_t[:], p2)
        load_k(1, 0)
        nc.sync.dma_start(out=xw_win[:].bitcast(I32), in_=x_words[0].rearrange("p n t -> p (n t)").bitcast(I32))
        for h in range(2):
            nc.sync.dma_start(out=w1_raw[h][:], in_=w1_rows[:, :, h * H // 2 : (h + 1) * H // 2])
        for t in range(1, 4):
            load_k(0, t)
            load_k(1, t)
        for t in range(4):
            nc.sync.dma_start(out=w2_raw[:, N * t : N * (t + 1)], in_=w2_rows[t])

        k_got = [[None] * 4, [None] * 4]

        def gather_k(s, t, on_vector=False, tag=None):
            k_got[s][t] = keep.tile([P, S], F32, name=f"k_got{s}_{t}", tag=tag or f"k_got{s}_{t}", align_bytes=64)
            window = k_win[s][t][:].indirect(cls_t[:])
            if on_vector:
                nc.vector.tensor_copy(k_got[s][t][:], window)
            else:
                nc.scalar.activation(k_got[s][t][:], window, COPY)

        xs_got = keep.tile([P, S], U8, name="xs_got", align_bytes=64)
        nc.vector.tensor_copy(xs_got[:], xs_win[:].indirect(offs_t[:]))
        for r in range(4):
            nc.scalar.dma_start(out=xq_scales[r:P:32, :].bitcast(I32), in_=xs_got[8 * r : P : 32, :].bitcast(I32))
        gather_k(0, 0, on_vector=True)
        gather_k(1, 0)
        xq_words = keep.tile([P, S], U32, name="xq_words", align_bytes=64)
        nc.vector.tensor_copy(xq_words[:], xw_win[:].indirect(offs_t[:]))

        w1_bf = keep.tile([P, 4, P, 4], BF16, name="w1_bf", align_bytes=64)

        def cast_w1(copy, h, g0, g1):
            copy(
                w1_bf[:, :, 64 * h + 4 * g0 : 64 * h + 4 * g1, :].rearrange("p t (g f) j -> p g t j f", f=4),
                w1_raw[h][:, :, 16 * g0 : 16 * g1].rearrange("p j (g t f) -> p g t j f", t=4, f=4),
            )

        cast_w1(nc.vector.tensor_copy, 0, 0, 16)
        cast_w1(nc.vector.tensor_copy, 1, 0, 10)
        cast_w1(nc.scalar.copy, 1, 10, 16)
        w1_codes, w1_scales = [], []
        for first, count in ((0, 1), (1, 3)):
            codes = keep.tile([P, count * P], U32, name=f"w1_codes{first}", tag=f"w1_codes{first}", align_bytes=64)
            scales = keep.tile([P, count * P], U8, name=f"w1_scales{first}", align_bytes=64)
            nc.vector.quantize_mx(
                out=codes[:].bitcast(FP8X4),
                scales=scales[:],
                in_=w1_bf[:, first : first + count].rearrange("p t m j -> p (t m j)"),
            )
            w1_codes.extend(codes[:, P * e : P * (e + 1)] for e in range(count))
            w1_scales.extend(scales[:, P * e : P * (e + 1)] for e in range(count))
        gather_k(0, 1)
        gather_k(1, 1, on_vector=True)

        y_win = [keep.tile([P, 2 * S if t < 2 else S], F32, name=f"y_win{t}", tag=f"y_win{t}") for t in range(4)]

        def project(t):
            bank = psum.tile([P, S], F32, name=f"y_bank{t}", tag=f"bank{t}")
            nc.tensor.matmul_mx(
                out=bank[:],
                lhsT=w1_codes[t].bitcast(FP8X4),
                lhsT_scale=w1_scales[t],
                rhs=xq_words[:].bitcast(FP8X4),
                rhs_scale=xq_scales[:],
                start=True,
                stop=True,
            )
            nc.scalar.copy(out=y_win[t][:, 0:S], in_=bank[:])

        project(0)
        project(1)
        gather_k(0, 2, tag="w1_codes0")
        project(2)
        gather_k(1, 2)
        project(3)
        gather_k(0, 3)
        gather_k(1, 3)

        taps = keep.tile([P, 8 * S - QUARTER + 2 * N], F32, name="taps", align_bytes=64)
        prods = [taps[:, 4 * S * (1 - s) : 4 * S * (2 - s)].rearrange("p (t n) -> p t n", t=4) for s in range(2)]
        w2_bf = taps[:, 8 * S - QUARTER : 8 * S - QUARTER + 2 * N].bitcast(BF16).rearrange("p (n j) -> p n j", j=4)
        z_rest = taps[:, 8 * S : 8 * S + 2 * HALF].bitcast(BF16).rearrange("p (n t) -> p n t", t=4)

        def neighbours(s, t, a, n):
            return y_win[t][:].indirect((p1_t, p2_t)[s][:, a // 16 : (a + n) // 16])

        def product(s, t, a, n):
            nc.vector.tensor_tensor(prods[s][:, t, a : a + n], neighbours(s, t, a, n), k_got[s][t][:, a : a + n], MULT)

        def add(z_bf, a, n):
            both = [prods[s][:, :, a : a + n].rearrange("p t (c i) -> p c t i", i=4) for s in range(2)]
            nc.vector.tensor_tensor(z_bf.rearrange("p (c i) t -> p c t i", i=4), both[0], both[1], ADD)

        def quantise(z_bf, a, n, z_codes):
            z_scales = keep.tile([P, n], U8, name=f"z_scales{a}", align_bytes=64)
            nc.vector.quantize_mx(out=z_codes.bitcast(FP8X4), scales=z_scales[:], in_=z_bf.rearrange("p n t -> p (n t)"))
            return z_codes, z_scales, a, n

        for t in range(2):
            for s in range(2):
                product(s, t, 0, S)
        for t in range(2, 4):
            for s in range(2):
                product(s, t, 0, HALF)
        product(1, 3, HALF, HALF)
        z_first = keep.tile([P, HALF, 4], BF16, name="z_first", align_bytes=64)
        add(z_first[:], 0, HALF)

        nc.scalar.copy(
            out=w2_bf.rearrange("p (c i) j -> p c j i", i=4),
            in_=w2_raw[:].rearrange("p (j c i) -> p c j i", j=4, i=4),
        )
        w2_codes = keep.tile([P, N], U32, name="w2_codes", align_bytes=64)
        w2_scales = keep.tile([P, N], U8, name="w2_scales", align_bytes=64)

        def quantise_w2(a, b):
            nc.vector.quantize_mx(
                out=w2_codes[:, a:b].bitcast(FP8X4), scales=w2_scales[:, a:b], in_=w2_bf[:, a:b, :].rearrange("p n j -> p (n j)")
            )

        first_codes = shared.tile([P, HALF], U32, name="first_codes", offset=4096, align_bytes=64)
        quantise_w2(0, N // 2)
        first = quantise(z_first[:], 0, HALF, first_codes[:])
        quantise_w2(N // 2, N)

        plain = ((0, 2), (1, 2), (0, 3))
        y_got = shared.tile([P, 2, 3, QUARTER], F32, name="y_got", offset=0, align_bytes=64)
        for b in range(2):
            for q, (s, t) in enumerate(plain[: 3 - b]):
                nc.scalar.activation(y_got[:, b, q, :], neighbours(s, t, HALF + QUARTER * b, QUARTER), COPY)

        def multiply(q, b):
            s, t = plain[q]
            places = slice(HALF + QUARTER * b, HALF + QUARTER * (b + 1))
            nc.vector.tensor_tensor(prods[s][:, t, places], y_got[:, b, q, :], k_got[s][t][:, places], MULT)

        out_rows = out.rearrange("(mt p) j -> p mt j", p=P)
        seen = []

        def leave(piece, parts, tag=None):
            z_codes, z_scales, a, n = piece
            tiles = [mt for part, bank, copy in parts for mt in part]
            res = keep.tile([P, len(tiles), n], F32, name=f"res{a}_{tiles[0]}", tag=tag or f"res{a}_{tiles[0]}")
            seen.append(res)
            for part, bank, copy in parts:
                acc = psum.tile([P, len(part), n], F32, name=f"acc{a}_{part[0]}", tag=f"bank{bank}")
                for q, mt in enumerate(part):
                    nc.tensor.matmul_mx(
                        out=acc[:, q, :],
                        lhsT=w2_codes[:, P * mt : P * (mt + 1)].bitcast(FP8X4),
                        lhsT_scale=w2_scales[:, P * mt : P * (mt + 1)],
                        rhs=z_codes.bitcast(FP8X4),
                        rhs_scale=z_scales[:],
                        start=True,
                        stop=True,
                    )
                copy(res[:, part[0] - tiles[0] : part[-1] - tiles[0] + 1, :], acc[:])
            nc.sync.dma_start(out=out_rows[:, tiles[0] : tiles[-1] + 1, a : a + n], in_=res[:])

        leave(first, [((0, 1), 4, nc.scalar.copy)], tag="y_win2")
        leave(first, [((2, 3), 5, nc.scalar.copy)])
        rest_codes = [keep.tile([P, QUARTER], U32, name=f"z_codes{b}", align_bytes=64) for b in range(2)]
        for q in range(3):
            multiply(q, 0)
        multiply(0, 1)
        add(z_rest[:, 0:QUARTER, :], HALF, QUARTER)
        multiply(1, 1)
        product(0, 3, HALF + QUARTER, QUARTER)
        middle = quantise(z_rest[:, 0:QUARTER, :], HALF, QUARTER, rest_codes[0][:])
        leave(middle, [((0, 1), 6, nc.scalar.copy)])
        leave(middle, [((2, 3), 3, nc.scalar.copy)])
        add(z_rest[:, QUARTER:HALF, :], HALF + QUARTER, QUARTER)
        last = quantise(z_rest[:, QUARTER:HALF, :], HALF + QUARTER, QUARTER, rest_codes[1][:])
        leave(last, [((0,), 7, nc.vector.tensor_copy), ((1,), 0, nc.scalar.copy)])
        leave(last, [((2,), 1, nc.vector.tensor_copy), ((3,), 2, nc.scalar.copy)])
